import numpy as np, ml_dtypes
CORES = [3,5,19,21,35,37,51,53,67,69]
N = 10
import mx_ref
BF = ml_dtypes.bfloat16
def entries(a):
    return np.ascontiguousarray(a.T).reshape(-1)
def table(e):
    return np.ascontiguousarray(np.reshape(e, (-1, 16)).T).astype(np.int32)
def cols(t, e):
    v = np.concatenate([t.reshape(128, -1, 4), np.zeros((128, 1, 4), BF)], axis=1)
    return np.ascontiguousarray(v[:, e]).reshape(128, -1)
def f(rng, *shape):
    return mx_ref.flush((rng.standard_normal(shape, dtype=np.float32) * np.exp2(rng.integers(-2, 3, shape[:-1] + (1,)))).astype(BF))
def wide(rng, *shape, cols=0):
    v = rng.standard_normal(shape, dtype=np.float32) * np.exp2(rng.integers(-12, 13, shape)).astype(np.float32)
    if cols: v *= np.repeat(np.exp2(rng.integers(-cols, cols + 1, shape[:-2] + (1, shape[-1] // 4))) * (rng.random(shape[:-2] + (1, shape[-1] // 4)) > 0.0625), 4, axis=-1).astype(np.float32)
    return mx_ref.flush(v.astype(BF))
T, NA, S, CAPP = 512, 256, 512, 64
def lists(rng, most=0, inorder=False, big=None):
    c, m = [], []
    for r in range(N):
        n = np.zeros(N, int)
        n[rng.permutation(N)[:most]] = CAPP
        while n.sum() < S:
            q = rng.integers(0, N)
            if n[q] < CAPP: n[q] += 1
        used = np.concatenate([q * CAPP + rng.permutation(CAPP)[:n[q]] for q in range(N)])
        slots = np.full(N * CAPP, -1); slots[used] = rng.integers(0, T, S)
        o = np.sort(used) if inorder else rng.permutation(used)
        if big is not None:
            for i in range(S // 32):
                k = o[32 * i + rng.integers(0, 32)]; slots[k] = rng.choice(big[k // CAPP])
        c.append(table(slots)); m.append(table(o))
    return {"want": np.stack(c), "slot": np.stack(m)}
def setup_inputs(rng):
    return {"v": f(rng, N, 128, 4 * T), "a": f(rng, N, 128, 4 * NA), **lists(rng)}
def setup_inputs_full(rng):
    return {**setup_inputs(rng), **lists(rng, most=S // CAPP)}
def setup_inputs_sorted(rng):
    return {**setup_inputs(rng), **lists(rng, inorder=True)}
def setup_inputs_giant(rng):
    d = setup_inputs(rng); big = [rng.permutation(T)[:T // 32] for q in range(N)]
    x = d["v"].reshape(N, 128, T, 4)
    for q in range(N): x[q][:, big[q]] = (x[q][:, big[q]].astype(np.float32) * np.float32(2.0 ** 20)).astype(BF)
    d["v"] = x.reshape(N, 128, 4 * T)
    return {**d, **lists(rng, big=big)}
def setup_inputs_spread(rng):
    d = setup_inputs(rng); d["v"] = wide(rng, N, 128, 4 * T); d["a"] = wide(rng, N, 128, 4 * NA); return d
def check_inputs(d):
    b = []
    for r in range(N):
        c, m = entries(d["want"][r]), entries(d["slot"][r])
        if c.min() < -1 or c.max() >= T or (c >= 0).sum() != S: b.append("want")
        if m.min() < 0 or m.max() >= N * CAPP or len(set(m.tolist())) != S or (c[np.clip(m, 0, N * CAPP - 1)] < 0).any(): b.append("slot")
    return b
def ones(b):
    e = np.zeros((128, 128, 4), np.float32); e[np.arange(128), np.arange(128), b] = 1
    return e.reshape(128, 512).astype(BF)
def decode(q):
    return np.stack([mx_ref.matmul(mx_ref.quantize(ones(b)), q) for b in range(4)], axis=1).reshape(512, -1)
def reference(v, a, want, slot, own=None):
    h = np.zeros((N, 128, 2048), BF); y = np.zeros((N, 128, 4 * NA), np.float32)
    for r in range(N):
        c = entries(want[r])
        arrived = np.concatenate([decode(mx_ref.quantize(cols(v[q], c[q * CAPP:(q + 1) * CAPP]))) for q in range(N)], axis=1)
        H = arrived[:, entries(slot[r])].T
        h[r] = H.reshape(128, 4, 512).transpose(0, 2, 1).reshape(128, 2048).astype(BF)
    for r in range(N):
        t = h[r] if own is None else np.asarray(own["h"][r])
        for o in range(4):
            y[r][:, NA * o:NA * o + NA] = mx_ref.matmul(mx_ref.quantize(np.ascontiguousarray(t[:, 512 * o:512 * o + 512])), mx_ref.quantize(a[r]))
    return {"y": y, "h": h}

@@ -1,0 +1,286 @@
+from concourse.bass import DstId, RemoteDMATransfer
+from concourse.mybir import dt, AluOpType, ActivationFunctionType
+
+BF, F32, I32, U16, CODE, U8 = "bfloat16", "float32", "int32", "uint16", "float8_e4m3fn_x4", "uint8"
+SCRATCH = {
+    "wl": ("sbuf", [128, 40], I32),
+    "sw": ("sbuf", [128, 32], I32),
+    "loff": ("sbuf", [128, 40], U16),
+    "lown": ("sbuf", [128, 4], U16),
+    "lst1": ("sbuf", [128, 16], U16),
+    "lst2": ("sbuf", [128, 20], U16),
+    "s1i": ("sbuf", [128, 32], I32),
+    "s2i": ("sbuf", [128, 32], I32),
+    "s3i": ("sbuf", [128, 32], I32),
+    "sl": ("sbuf", [128, 32], U16),
+    "vt": ("sbuf", [128, 2048], BF),
+    "at": ("sbuf", [128, 1024], BF),
+    "gt1": ("sbuf", [128, 1024], BF),
+    "gt2": ("sbuf", [128, 1536], BF),
+    "e1": ("sbuf", [128, 512], BF),
+    "e2": ("sbuf", [128, 4], F32),
+    "e3": ("sbuf", [128, 128], F32),
+    "idt": ("sbuf", [128, 2048], BF),
+    "idn": ("sbuf", [128, 128], F32),
+    "eq": ("sbuf", [128, 512], CODE), "eqs": ("sbuf", [128, 512], U8),
+    "aq": ("sbuf", [128, 256], CODE), "aqs": ("sbuf", [128, 256], U8),
+    "k1": ("sbuf", [128, 256], CODE), "k1s": ("sbuf", [128, 256], U8),
+    "k2": ("sbuf", [128, 512], CODE), "k2s": ("sbuf", [128, 512], U8),
+    "r1": ("sbuf", [128, 256], CODE), "r1s": ("sbuf", [128, 256], U8),
+    "r2": ("sbuf", [128, 256], CODE), "r2s": ("sbuf", [128, 256], U8),
+    "hq": ("sbuf", [128, 512], CODE), "hqs": ("sbuf", [128, 512], U8),
+    "w": ("sbuf", [128, 2560], F32),
+    "gg": ("sbuf", [128, 2048], F32),
+    "ht": ("sbuf", [128, 2048], BF),
+    "yt": ("sbuf", [128, 1024], F32),
+    "pu": ("psum", [128, 2560], F32),
+    "py": ("psum", [128, 1536], F32),
+}
+SEMAPHORES = (["ld_w", "ld_v", "ld_a", "ld_s", "it1", "it2", "it3", "cv", "cvo", "eb", "eqd", "gov", "gos", "l1", "l2",
+               "g1v", "g1s", "q1", "g2v", "g2s", "q2", "qa", "sa", "sb", "sc", "sl", "idn", "arr1", "arr2", "arrn",
+               "sent", "stored"]
+              + ["%s%d" % (n, b) for n in ("mb1_", "mb0_", "mb2_", "cb1_", "cb0_", "cb2_", "gv", "gs", "tr", "tt", "hc", "hp",
+                                           "hq", "ym", "yc") for b in range(4)])
+OTHER = {"v": "s", "s": "v"}
+
+
+def rank_program(g, core, T, topo):
+    rank = T.rank_of(core)
+    if rank is None:
+        return
+    V, S, PE, SY = g.vector, g.scalar, g.tensor, g.sync
+    sem = T.sem
+    COPY = ActivationFunctionType.Copy
+    chips = []
+    for c in T.cores:
+        if topo.chip(c) not in chips:
+            chips.append(topo.chip(c))
+    members = [[T.rank_of(c) for c in T.cores if topo.chip(c) == ch] for ch in chips]
+    nch = len(chips)
+    me = chips.index(topo.chip(core))
+    par = members[me].index(rank)
+    nbr = members[me][1 - par]
+
+    def at(d):
+        return members[(me + d) % nch]
+
+    for q, lo in ((SY, 0), (S, 4)):
+        for k in range(lo, lo + 4):
+            q.dma_start(T.wl[16 * k:16 * k + 16, :], T.want[:, :]).then_inc(sem["ld_w"], 16)
+    SY.dma_start(T.vt[:, :], T.v[:, :]).then_inc(sem["ld_v"], 16)
+    for q, lo in ((SY, 0), (S, 4)):
+        for k in range(lo, lo + 4):
+            q.dma_start(T.sw[16 * k:16 * k + 16, :], T.slot[:, :]).then_inc(sem["ld_s"], 16)
+    SY.dma_start(T.at[:, :], T.a[:, :]).then_inc(sem["ld_a"], 16)
+
+    g.iota(T.e2[:, :], [[-128, 4]], 0, 4, allow_small_or_imprecise_dtypes=True).then_inc(sem["it2"], 1)
+    g.iota(T.e1[:, :], [[1, 128], [-1, 4]], 0, 0, allow_small_or_imprecise_dtypes=True).then_inc(sem["it1"], 1)
+    g.iota(T.e3[:, :], [[1, 128]], 0, -1, allow_small_or_imprecise_dtypes=True).then_inc(sem["it3"], 1)
+
+    off_ranks = at(1) + at(2) + at(3) + at(4)
+    off_eng = topo.engines(core, T.cores[off_ranks[0]])
+    share = len(off_eng) // 4
+    masks = [sum(1 << e for e in off_eng[share * m:share * m + share]) for m in range(4)]
+    spare = [e for e in topo.engines(core, T.cores[nbr]) if e not in off_eng]
+    masks.append(sum(1 << e for e in spare[::2][:share]))
+
+    def send(items):
+        trs = []
+        for r, m, s, d, x in items:
+            rid, pid, _ = topo.addr(T.cores[r])
+            trs.append(RemoteDMATransfer(dst_ids=[DstId(rid=rid, pnc=pid)], dma_engine_mask=masks[m], remote_sem=sem[s],
+                                         srcs=[x], dsts=[d], alu_op=0))
+        g.remote_dma_fused(trs, local_sem=sem["sent"])
+
+    g.wait_ge(sem["cv"], 1)
+    send([(r, 2 * i + j, "l1", T.lst1[:, 8 * i + 4 * par:8 * i + 4 * par + 4], T.loff[:, 4 * r:4 * r + 4])
+          for i, d in enumerate((-1, -2)) for j, r in enumerate(at(d))])
+    send([(r, 2 * i + j, "l2", T.lst2[:, 8 * i + 4 * par:8 * i + 4 * par + 4], T.loff[:, 4 * r:4 * r + 4])
+          for i, d in enumerate((-3, -4)) for j, r in enumerate(at(d))]
+         + [(nbr, 4, "l2", T.lst2[:, 16:20], T.loff[:, 4 * nbr:4 * nbr + 4])])
+
+    to1 = [(r, 2 * i + j, 128 * (1 - i) + 64 * par, 128 * i + 64 * j) for i, d in enumerate((1, 2)) for j, r in enumerate(at(d))]
+    g.wait_ge(sem["q1"], 1)
+    send([(r, m, "arr1", T.r1[:, d:d + 64].bitcast(dt.uint8), T.k1[:, x:x + 64].bitcast(dt.uint8)) for r, m, d, x in to1])
+    send([(r, m, "arr1", T.r1s[:, d:d + 64], T.k1s[:, x:x + 64]) for r, m, d, x in to1])
+    base = 64 + 64 * par
+    own = 384 if par == 0 else 64
+    pair = 384 if par == 0 else 0
+    nland = 448 if par == 1 else 0
+    to2 = [(r, 2 * i + j, 128 * (1 - i) + 64 * par, base + 128 * i + 64 * j) for i, d in enumerate((3, 4)) for j, r in enumerate(at(d))]
+    g.wait_ge(sem["q2"], 1)
+    send([(r, m, "arr2", T.r2[:, d:d + 64].bitcast(dt.uint8), T.k2[:, x:x + 64].bitcast(dt.uint8)) for r, m, d, x in to2]
+         + [(nbr, 4, "arrn", T.k2[:, nland:nland + 64].bitcast(dt.uint8), T.k2[:, base + 256:base + 320].bitcast(dt.uint8))])
+    send([(r, m, "arr2", T.r2s[:, d:d + 64], T.k2s[:, x:x + 64]) for r, m, d, x in to2]
+         + [(nbr, 4, "arrn", T.k2s[:, nland:nland + 64], T.k2s[:, base + 256:base + 320])])
+    g.wait_ge(sem["sent"], share * (4 + 5 + 4 + 4 + 5 + 5))
+
+    def copy(q, out, in_, s):
+        if q == "v":
+            V.tensor_copy(out, in_).then_inc(sem[s], 1)
+        else:
+            S.activation(out, in_, COPY).then_inc(sem[s], 1)
+
+    def wait(q, *pairs):
+        for s, n in pairs:
+            (V if q == "v" else S).wait_ge(sem[s], n)
+
+    wait("v", ("ld_w", 128))
+    V.tensor_scalar(T.loff[:, :], T.wl[:, :], 0, 4, AluOpType.max, AluOpType.mult).then_inc(sem["cv"], 1)
+    V.tensor_scalar(T.lown[:, :], T.wl[:, 4 * rank:4 * rank + 4], 0, 4, AluOpType.max, AluOpType.mult).then_inc(sem["cvo"], 1)
+    wait("v", ("it1", 1), ("it2", 1))
+    for b in range(4):
+        V.tensor_scalar(T.idt[:, 512 * b:512 * b + 512], T.e1[:, :], T.e2[:, b:b + 1], None, AluOpType.is_equal).then_inc(sem["eb"], 1)
+    wait("v", ("eb", 4))
+    V.quantize_mx(T.eq[:, :], T.eqs[:, :], T.idt[:, :]).then_inc(sem["eqd"], 1)
+
+    goff = 0 if par == 0 else 64
+    gown = 320 if par == 0 else 0
+    for q, ts in (("v", (0, 1)), ("s", (2, 3))):
+        wait(q, ("ld_v", 16), ("cvo", 1))
+        for t in ts:
+            copy(q, T.gt2[:, 4 * gown + t:4 * gown + 256:4], T.vt[:, t:2048].indirect(T.lown[:, 0:4]), "go" + q)
+        wait(q, ("l1", 4 * share))
+        for t in ts:
+            copy(q, T.gt1[:, t:1024:4], T.vt[:, t:2048].indirect(T.lst1[:, 0:16]), "g1" + q)
+        if q == "v":
+            wait("v", ("g1v", 2), ("g1s", 2))
+            V.quantize_mx(T.k1[:, :], T.k1s[:, :], T.gt1[:, :]).then_inc(sem["q1"], 1)
+        wait(q, ("l2", 5 * share))
+        for t in ts:
+            copy(q, T.gt2[:, 4 * goff + t:4 * goff + 1280:4], T.vt[:, t:2048].indirect(T.lst2[:, 0:20]), "g2" + q)
+    wait("v", ("gov", 2), ("gos", 2), ("g2v", 2), ("g2s", 2))
+    V.quantize_mx(T.k2[:, 64:448], T.k2s[:, 64:448], T.gt2[:, :]).then_inc(sem["q2"], 1)
+
+    wait("v", ("ld_a", 16))
+    V.quantize_mx(T.aq[:, :], T.aqs[:, :], T.at[:, :]).then_inc(sem["qa"], 1)
+    wait("v", ("ld_s", 128))
+    V.tensor_scalar(T.s1i[:, :], T.sw[:, :], 128 * me, 640, AluOpType.is_lt, AluOpType.mult).then_inc(sem["sa"], 1)
+    V.tensor_scalar(T.s2i[:, :], T.sw[:, :], 128 * me, None, AluOpType.subtract).then_inc(sem["sb"], 1)
+    wait("v", ("it3", 1))
+    V.tensor_scalar(T.idn[:, :], T.e3[:, :], 0.0, None, AluOpType.is_equal).then_inc(sem["idn"], 1)
+    wait("v", ("sa", 1), ("sb", 1))
+    V.tensor_tensor(T.s3i[:, :], T.s1i[:, :], T.s2i[:, :], AluOpType.add).then_inc(sem["sc"], 1)
+    wait("v", ("sc", 1))
+    V.tensor_copy(T.sl[:, :], T.s3i[:, :]).then_inc(sem["sl"], 1)
+
+    bank0, bank2, bankt = (4, 0, 1, 2), (3, 4, 0, 1), (2, 3, 4)
+
+    def P(k, n):
+        return T.pu[:, 512 * k:512 * k + n]
+
+    def E(b):
+        return T.eq[:, 128 * b:128 * b + 128], T.eqs[:, 128 * b:128 * b + 128]
+
+    PE.wait_ge(sem["eqd"], 1)
+    PE.wait_ge(sem["arr1"], 8 * share)
+    for b in range(4):
+        PE.matmul_mx(P(b, 256), *E(b), T.r1[:, :], T.r1s[:, :], True, True).then_inc(sem["mb1_%d" % b], 1)
+    PE.wait_ge(sem["q2"], 1)
+    PE.wait_ge(sem["arrn"], 2 * share)
+    for b in range(4):
+        if b:
+            PE.wait_ge(sem["cb1_%d" % (b - 1)], 1)
+        PE.matmul_mx(P(bank0[b], 128), *E(b), T.k2[:, pair:pair + 128], T.k2s[:, pair:pair + 128], True, True).then_inc(sem["mb0_%d" % b], 1)
+    PE.wait_ge(sem["arr2"], 8 * share)
+    for b in range(4):
+        PE.wait_ge(sem["cb1_3"] if b == 0 else sem["cb0_%d" % (b - 1)], 1)
+        PE.matmul_mx(P(bank2[b], 256), *E(b), T.r2[:, :], T.r2s[:, :], True, True).then_inc(sem["mb2_%d" % b], 1)
+    PE.wait_ge(sem["idn"], 1)
+    PE.wait_ge(sem["qa"], 1)
+
+    def product(o, k):
+        PE.wait_ge(sem["hq%d" % o], 1)
+        PE.matmul_mx(T.py[:, 512 * k:512 * k + 256], T.hq[:, 128 * o:128 * o + 128], T.hqs[:, 128 * o:128 * o + 128],
+                     T.aq[:, :], T.aqs[:, :], True, True).then_inc(sem["ym%d" % o], 1)
+
+    for o in range(3):
+        PE.wait_ge(sem["gv%d" % o], 1)
+        PE.wait_ge(sem["gs%d" % o], 1)
+        PE.wait_ge(sem["cb0_3"] if o == 0 else sem["cb2_%d" % (o - 1)], 1)
+        for t in range(4):
+            PE.transpose(T.pu[:, 512 * bankt[o] + t:512 * bankt[o] + 512:4], T.gg[:, 512 * o + t:512 * o + 512:4], T.idn[:, :]).then_inc(sem["tr%d" % o], 1)
+    PE.wait_ge(sem["gv3"], 1)
+    PE.wait_ge(sem["gs3"], 1)
+    for t in range(4):
+        PE.wait_ge(sem[("cb2_2", "cb2_3", "hc0", "hc1")[t]], 1)
+        PE.transpose(P(t, 128), T.gg[:, 1536 + t:2048:4], T.idn[:, :]).then_inc(sem["tt%d" % t], 1)
+        if t == 1:
+            product(0, 0)
+    product(1, 1)
+    product(2, 2)
+    PE.wait_ge(sem["yc0"], 1)
+    product(3, 0)
+
+    def towin(q, b):
+        for n, banks, first, width in (("b1_", (0, 1, 2, 3), 384, 256), ("b0_", bank0, 0, 128)):
+            pass
+
+    def unpacked(q, n, b, bank, first, width):
+        wait(q, ("m%s%d" % (n, b), 1))
+        copy(q, T.w[:, 640 * b + first:640 * b + first + width], P(bank, width), "c%s%d" % (n, b))
+
+    def choose(q, o):
+        wait(q, ("sl", 1), ("cb1_%d" % o, 1), ("cb0_%d" % o, 1), ("cb2_%d" % o, 1))
+        k = 0 if q == "v" else 1
+        copy(q, T.gg[:, 512 * o + 256 * k:512 * o + 256 * k + 256], T.w[:, 640 * o:640 * o + 640].indirect(T.sl[:, 16 * k:16 * k + 16]), "g%s%d" % (q, o))
+
+    def block(q, o):
+        wait(q, ("tr%d" % o, 4))
+        copy(q, T.ht[:, 512 * o:512 * o + 512], P(bankt[o], 512), "hc%d" % o)
+
+    def piece(q, t):
+        wait(q, ("tt%d" % t, 1))
+        copy(q, T.ht[:, 1536 + t:2048:4], P(t, 128), "hp%d" % t)
+
+    def quant(o):
+        wait("v", *([("hc%d" % o, 1)] if o < 3 else [("hp%d" % t, 1) for t in range(4)]))
+        V.quantize_mx(T.hq[:, 128 * o:128 * o + 128], T.hqs[:, 128 * o:128 * o + 128], T.ht[:, 512 * o:512 * o + 512]).then_inc(sem["hq%d" % o], 1)
+
+    def result(q, o, k):
+        wait(q, ("ym%d" % o, 1))
+        copy(q, T.yt[:, 256 * o:256 * o + 256], T.py[:, 512 * k:512 * k + 256], "yc%d" % o)
+
+    for q, bs in (("v", (0, 2)), ("s", (1, 3))):
+        for b in bs:
+            unpacked(q, "b1_", b, b, 384, 256)
+        for b in bs:
+            unpacked(q, "b0_", b, bank0[b], 0, 128)
+        for o, b in ((0, bs[0]), (1, bs[1])):
+            unpacked(q, "b2_", b, bank2[b], 128, 256)
+            choose(q, o)
+        choose(q, 2)
+        choose(q, 3)
+    block("v", 1)
+    block("s", 0)
+    quant(0)
+    quant(1)
+    block("s", 2)
+    quant(2)
+    piece("s", 0)
+    result("s", 0, 0)
+    piece("s", 2)
+    piece("v", 1)
+    piece("v", 3)
+    quant(3)
+    result("v", 1, 1)
+    result("s", 2, 2)
+    result("v", 3, 0)
+
+    def store_h(o):
+        for s in (["hc%d" % o] if o < 3 else ["hp%d" % t for t in range(4)]):
+            SY.wait_ge(sem[s], 1)
+        SY.dma_start(T.h[:, 512 * o:512 * o + 512], T.ht[:, 512 * o:512 * o + 512]).then_inc(sem["stored"], 16)
+
+    def store_y(o):
+        SY.wait_ge(sem["yc%d" % o], 1)
+        SY.dma_start(T.y[:, 256 * o:256 * o + 256], T.yt[:, 256 * o:256 * o + 256]).then_inc(sem["stored"], 16)
+
+    store_h(0)
+    store_h(1)
+    store_h(2)
+    store_y(0)
+    store_h(3)
+    for o in (1, 2, 3):
+        store_y(o)
+    SY.wait_ge(sem["stored"], 128)

@@ -2,46 +2,50 @@ from concourse.bass import DstId, RemoteDMATransfer
 from concourse.mybir import dt, AluOpType, ActivationFunctionType
 
 BF, F32, I32, U16, CODE, U8 = "bfloat16", "float32", "int32", "uint16", "float8_e4m3fn_x4", "uint8"
+BATCHES = ((1,), (2, 3), (4,))
+LISTS = ((1, 2), (3, 4))
+HELP = (0, 96, 64)
+NB = len(BATCHES)
 SCRATCH = {
     "wl": ("sbuf", [128, 40], I32),
     "sw": ("sbuf", [128, 32], I32),
     "loff": ("sbuf", [128, 40], U16),
-    "lown": ("sbuf", [128, 4], U16),
-    "lst1": ("sbuf", [128, 16], U16),
-    "lst2": ("sbuf", [128, 20], U16),
+    "lst": ("sbuf", [128, 40], U16),
     "s1i": ("sbuf", [128, 32], I32),
     "s2i": ("sbuf", [128, 32], I32),
-    "s3i": ("sbuf", [128, 32], I32),
     "sl": ("sbuf", [128, 32], U16),
+    "slx": ("sbuf", [128, 64], U16),
     "vt": ("sbuf", [128, 2048], BF),
     "at": ("sbuf", [128, 1024], BF),
-    "gt1": ("sbuf", [128, 1024], BF),
-    "gt2": ("sbuf", [128, 1536], BF),
-    "e1": ("sbuf", [128, 512], BF),
-    "e2": ("sbuf", [128, 4], F32),
-    "e3": ("sbuf", [128, 128], F32),
+    "ea": ("sbuf", [128, 128], BF), "eb": ("sbuf", [128, 128], BF), "ec": ("sbuf", [128, 2], BF),
     "idt": ("sbuf", [128, 2048], BF),
     "idn": ("sbuf", [128, 128], F32),
     "eq": ("sbuf", [128, 512], CODE), "eqs": ("sbuf", [128, 512], U8),
     "aq": ("sbuf", [128, 256], CODE), "aqs": ("sbuf", [128, 256], U8),
-    "k1": ("sbuf", [128, 256], CODE), "k1s": ("sbuf", [128, 256], U8),
-    "k2": ("sbuf", [128, 512], CODE), "k2s": ("sbuf", [128, 512], U8),
-    "r1": ("sbuf", [128, 256], CODE), "r1s": ("sbuf", [128, 256], U8),
-    "r2": ("sbuf", [128, 256], CODE), "r2s": ("sbuf", [128, 256], U8),
     "hq": ("sbuf", [128, 512], CODE), "hqs": ("sbuf", [128, 512], U8),
-    "w": ("sbuf", [128, 2560], F32),
-    "gg": ("sbuf", [128, 2048], F32),
+    "w": ("sbuf", [128, 2560], BF),
+    "gg": ("sbuf", [128, 1024], F32),
+    "gd": ("sbuf", [128, 1024], BF),
+    "xd": ("sbuf", [128, 1024], BF),
     "ht": ("sbuf", [128, 2048], BF),
     "yt": ("sbuf", [128, 1024], F32),
-    "pu": ("psum", [128, 2560], F32),
-    "py": ("psum", [128, 1536], F32),
+    "ps": ("psum", [128, 4096], F32),
 }
-SEMAPHORES = (["ld_w", "ld_v", "ld_a", "ld_s", "it1", "it2", "it3", "cv", "cvo", "eb", "eqd", "gov", "gos", "l1", "l2",
-               "g1v", "g1s", "q1", "g2v", "g2s", "q2", "qa", "sa", "sb", "sc", "sl", "idn", "arr1", "arr2", "arrn",
-               "sent", "stored"]
-              + ["%s%d" % (n, b) for n in ("mb1_", "mb0_", "mb2_", "cb1_", "cb0_", "cb2_", "gv", "gs", "tr", "tt", "hc", "hp",
-                                           "hq", "ym", "yc") for b in range(4)])
-OTHER = {"v": "s", "s": "v"}
+for _b, _ds in enumerate(BATCHES):
+    _n = 128 * len(_ds)
+    _x = 128 if _b == NB - 1 else 0
+    SCRATCH["gt%d" % _b] = ("sbuf", [128, 4 * (_n + _x)], BF)
+    SCRATCH["k%d" % _b] = ("sbuf", [128, _n + 2 * _x], CODE)
+    SCRATCH["ks%d" % _b] = ("sbuf", [128, _n + 2 * _x], U8)
+    SCRATCH["r%d" % _b] = ("sbuf", [128, _n], CODE)
+    SCRATCH["rs%d" % _b] = ("sbuf", [128, _n], U8)
+SEMAPHORES = (["ld_w", "ld_v", "ld_a", "ld_s", "ita", "itb", "itc", "cv", "eb", "eqd", "go", "qa", "sa", "sb", "sl", "idn",
+               "arrn", "sent", "stored", "xd"]
+              + ["l%d" % i for i in range(len(LISTS))]
+              + ["%s%d" % (n, b) for n in ("gav", "gas", "q", "arr") for b in range(NB)]
+              + ["%s%d_%d" % (n, b, o) for n in ("m", "c") for b in range(NB + 1) for o in range(4)]
+              + ["%s%d" % (n, b) for n in ("gd", "tt", "hp", "hc", "hq", "ym", "yc") for b in range(4)]
+              + ["gv2", "gs2", "gv3", "gs3", "tr2"])
 
 
 def rank_program(g, core, T, topo):
@@ -50,6 +54,7 @@ def rank_program(g, core, T, topo):
         return
     V, S, PE, SY = g.vector, g.scalar, g.tensor, g.sync
     sem = T.sem
+    A = AluOpType
     COPY = ActivationFunctionType.Copy
     chips = []
     for c in T.cores:
@@ -60,6 +65,7 @@ def rank_program(g, core, T, topo):
     me = chips.index(topo.chip(core))
     par = members[me].index(rank)
     nbr = members[me][1 - par]
+    last = NB - 1
 
     def at(d):
         return members[(me + d) % nch]
@@ -68,52 +74,60 @@ def rank_program(g, core, T, topo):
         for k in range(lo, lo + 4):
             q.dma_start(T.wl[16 * k:16 * k + 16, :], T.want[:, :]).then_inc(sem["ld_w"], 16)
     SY.dma_start(T.vt[:, :], T.v[:, :]).then_inc(sem["ld_v"], 16)
+    SY.dma_start(T.at[:, :], T.a[:, :]).then_inc(sem["ld_a"], 16)
     for q, lo in ((SY, 0), (S, 4)):
         for k in range(lo, lo + 4):
             q.dma_start(T.sw[16 * k:16 * k + 16, :], T.slot[:, :]).then_inc(sem["ld_s"], 16)
-    SY.dma_start(T.at[:, :], T.a[:, :]).then_inc(sem["ld_a"], 16)
 
-    g.iota(T.e2[:, :], [[-128, 4]], 0, 4, allow_small_or_imprecise_dtypes=True).then_inc(sem["it2"], 1)
-    g.iota(T.e1[:, :], [[1, 128], [-1, 4]], 0, 0, allow_small_or_imprecise_dtypes=True).then_inc(sem["it1"], 1)
-    g.iota(T.e3[:, :], [[1, 128]], 0, -1, allow_small_or_imprecise_dtypes=True).then_inc(sem["it3"], 1)
+    g.iota(T.ec[:, :], [[0, 2]], 0, 4, allow_small_or_imprecise_dtypes=True).then_inc(sem["itc"], 1)
+    g.iota(T.ea[:, :], [[1, 128]], 0, 0, allow_small_or_imprecise_dtypes=True).then_inc(sem["ita"], 1)
+    g.iota(T.eb[:, :], [[1, 32], [64, 4]], 0, 0, allow_small_or_imprecise_dtypes=True).then_inc(sem["itb"], 1)
 
-    off_ranks = at(1) + at(2) + at(3) + at(4)
-    off_eng = topo.engines(core, T.cores[off_ranks[0]])
-    share = len(off_eng) // 4
-    masks = [sum(1 << e for e in off_eng[share * m:share * m + share]) for m in range(4)]
-    spare = [e for e in topo.engines(core, T.cores[nbr]) if e not in off_eng]
-    masks.append(sum(1 << e for e in spare[::2][:share]))
+    off_eng = topo.engines(core, T.cores[at(1)[0]])
+    spare = [e for e in topo.engines(core, T.cores[nbr]) if e not in off_eng][::2]
 
-    def send(items):
+    def share(ds):
+        return len(off_eng) // (2 * len(ds))
+
+    nshare = min(share(BATCHES[last]), len(spare))
+    sent = [0]
+
+    def send(ds, items, to_nbr=None):
+        n = share(ds)
+        sets = [off_eng[n * m:n * m + n] for m in range(len(items))]
+        if to_nbr:
+            items, sets = items + [to_nbr], sets + [spare[:nshare]]
         trs = []
-        for r, m, s, d, x in items:
+        for (r, s, d, x), es in zip(items, sets):
             rid, pid, _ = topo.addr(T.cores[r])
-            trs.append(RemoteDMATransfer(dst_ids=[DstId(rid=rid, pnc=pid)], dma_engine_mask=masks[m], remote_sem=sem[s],
-                                         srcs=[x], dsts=[d], alu_op=0))
+            trs.append(RemoteDMATransfer(dst_ids=[DstId(rid=rid, pnc=pid)], dma_engine_mask=sum(1 << e for e in es),
+                                         remote_sem=sem[s], srcs=[x], dsts=[d], alu_op=0))
+            sent[0] += len(es)
         g.remote_dma_fused(trs, local_sem=sem["sent"])
 
     g.wait_ge(sem["cv"], 1)
-    send([(r, 2 * i + j, "l1", T.lst1[:, 8 * i + 4 * par:8 * i + 4 * par + 4], T.loff[:, 4 * r:4 * r + 4])
-          for i, d in enumerate((-1, -2)) for j, r in enumerate(at(d))])
-    send([(r, 2 * i + j, "l2", T.lst2[:, 8 * i + 4 * par:8 * i + 4 * par + 4], T.loff[:, 4 * r:4 * r + 4])
-          for i, d in enumerate((-3, -4)) for j, r in enumerate(at(d))]
-         + [(nbr, 4, "l2", T.lst2[:, 16:20], T.loff[:, 4 * nbr:4 * nbr + 4])])
+    for i, ds in enumerate(LISTS):
+        s = "l%d" % i
+        send(ds, [(r, s, T.lst[:, 8 * d - 8 + 4 * par:8 * d - 4 + 4 * par], T.loff[:, 4 * r:4 * r + 4]) for d in ds for r in at(-d)],
+             (nbr, s, T.lst[:, 32:36], T.loff[:, 4 * nbr:4 * nbr + 4]) if i == len(LISTS) - 1 else None)
+    lcount = [len(off_eng) + (nshare if i == len(LISTS) - 1 else 0) for i in range(len(LISTS))]
 
-    to1 = [(r, 2 * i + j, 128 * (1 - i) + 64 * par, 128 * i + 64 * j) for i, d in enumerate((1, 2)) for j, r in enumerate(at(d))]
-    g.wait_ge(sem["q1"], 1)
-    send([(r, m, "arr1", T.r1[:, d:d + 64].bitcast(dt.uint8), T.k1[:, x:x + 64].bitcast(dt.uint8)) for r, m, d, x in to1])
-    send([(r, m, "arr1", T.r1s[:, d:d + 64], T.k1s[:, x:x + 64]) for r, m, d, x in to1])
+    nl = 128 * len(BATCHES[last])
     base = 64 + 64 * par
-    own = 384 if par == 0 else 64
-    pair = 384 if par == 0 else 0
-    nland = 448 if par == 1 else 0
-    to2 = [(r, 2 * i + j, 128 * (1 - i) + 64 * par, base + 128 * i + 64 * j) for i, d in enumerate((3, 4)) for j, r in enumerate(at(d))]
-    g.wait_ge(sem["q2"], 1)
-    send([(r, m, "arr2", T.r2[:, d:d + 64].bitcast(dt.uint8), T.k2[:, x:x + 64].bitcast(dt.uint8)) for r, m, d, x in to2]
-         + [(nbr, 4, "arrn", T.k2[:, nland:nland + 64].bitcast(dt.uint8), T.k2[:, base + 256:base + 320].bitcast(dt.uint8))])
-    send([(r, m, "arr2", T.r2s[:, d:d + 64], T.k2s[:, x:x + 64]) for r, m, d, x in to2]
-         + [(nbr, 4, "arrn", T.k2s[:, nland:nland + 64], T.k2s[:, base + 256:base + 320])])
-    g.wait_ge(sem["sent"], share * (4 + 5 + 4 + 4 + 5 + 5))
+    pair = nl + 128 if par == 0 else 0
+    nland = nl + 192 if par == 1 else 0
+    for b, ds in enumerate(BATCHES):
+        x0 = base if b == last else 0
+        to = [(r, 128 * (len(ds) - 1 - i) + 64 * par, x0 + 128 * i + 64 * j) for i, d in enumerate(ds) for j, r in enumerate(at(d))]
+        g.wait_ge(sem["q%d" % b], 1)
+        for k, r_, cast in (("k", "r", True), ("ks", "rs", False)):
+            K, R_ = T["%s%d" % (k, b)], T["%s%d" % (r_, b)]
+
+            def view(buf, c):
+                return buf[:, c:c + 64].bitcast(dt.uint8) if cast else buf[:, c:c + 64]
+            send(ds, [(r, "arr%d" % b, view(R_, d), view(K, x)) for r, d, x in to],
+                 (nbr, "arrn", view(K, nland), view(K, base + nl)) if b == last else None)
+    g.wait_ge(sem["sent"], sent[0])
 
     def copy(q, out, in_, s):
         if q == "v":
@@ -125,162 +139,194 @@ def rank_program(g, core, T, topo):
         for s, n in pairs:
             (V if q == "v" else S).wait_ge(sem[s], n)
 
+    def ones(o):
+        for t in range(4):
+            V.tensor_scalar(T.idt[:, 512 * o + t:512 * o + 512:4], (T.eb if o < 2 else T.ea)[:, :], float((32 if o < 2 else 128) * o - t),
+                            T.ec[:, 0:1], A.add, A.is_equal).then_inc(sem["eb"], 1)
+
+    wait("v", ("itc", 1), ("ita", 1))
+    ones(2)
     wait("v", ("ld_w", 128))
-    V.tensor_scalar(T.loff[:, :], T.wl[:, :], 0, 4, AluOpType.max, AluOpType.mult).then_inc(sem["cv"], 1)
-    V.tensor_scalar(T.lown[:, :], T.wl[:, 4 * rank:4 * rank + 4], 0, 4, AluOpType.max, AluOpType.mult).then_inc(sem["cvo"], 1)
-    wait("v", ("it1", 1), ("it2", 1))
-    for b in range(4):
-        V.tensor_scalar(T.idt[:, 512 * b:512 * b + 512], T.e1[:, :], T.e2[:, b:b + 1], None, AluOpType.is_equal).then_inc(sem["eb"], 1)
-    wait("v", ("eb", 4))
+    V.tensor_scalar(T.loff[:, :], T.wl[:, :], 0, 4, A.max, A.mult).then_inc(sem["cv"], 1)
+    ones(3)
+    wait("v", ("itb", 1))
+    ones(0)
+    ones(1)
+    V.tensor_scalar(T.idn[:, :], T.ea[:, :], 4.0, T.ec[:, 0:1], A.mult, A.is_equal).then_inc(sem["idn"], 1)
+    wait("v", ("eb", 16))
     V.quantize_mx(T.eq[:, :], T.eqs[:, :], T.idt[:, :]).then_inc(sem["eqd"], 1)
 
-    goff = 0 if par == 0 else 64
-    gown = 320 if par == 0 else 0
-    for q, ts in (("v", (0, 1)), ("s", (2, 3))):
-        wait(q, ("ld_v", 16), ("cvo", 1))
-        for t in ts:
-            copy(q, T.gt2[:, 4 * gown + t:4 * gown + 256:4], T.vt[:, t:2048].indirect(T.lown[:, 0:4]), "go" + q)
-        wait(q, ("l1", 4 * share))
-        for t in ts:
-            copy(q, T.gt1[:, t:1024:4], T.vt[:, t:2048].indirect(T.lst1[:, 0:16]), "g1" + q)
-        if q == "v":
-            wait("v", ("g1v", 2), ("g1s", 2))
-            V.quantize_mx(T.k1[:, :], T.k1s[:, :], T.gt1[:, :]).then_inc(sem["q1"], 1)
-        wait(q, ("l2", 5 * share))
-        for t in ts:
-            copy(q, T.gt2[:, 4 * goff + t:4 * goff + 1280:4], T.vt[:, t:2048].indirect(T.lst2[:, 0:20]), "g2" + q)
-    wait("v", ("gov", 2), ("gos", 2), ("g2v", 2), ("g2s", 2))
-    V.quantize_mx(T.k2[:, 64:448], T.k2s[:, 64:448], T.gt2[:, :]).then_inc(sem["q2"], 1)
+    goff = 64 * par
+    gown = nl + 64 if par == 0 else 0
+    wait("s", ("ld_v", 16), ("cv", 1))
+    for t in range(4):
+        copy("s", T["gt%d" % last][:, 4 * gown + t:4 * gown + 256:4], T.vt[:, t:2048].indirect(T.loff[:, 4 * rank:4 * rank + 4]), "go")
+    wait("v", ("ld_v", 16))
+    for b, ds in enumerate(BATCHES):
+        n = 128 * len(ds) + (64 if b == last else 0)
+        c0 = goff if b == last else 0
+        l0 = 8 * ds[0] - 8
+        need = [("l%d" % i, lcount[i]) for i, ls in enumerate(LISTS) if set(ls) & set(ds) or (b == last and i == len(LISTS) - 1)]
+        cut = n - HELP[b]
+        parts = {"v": [(0, 0, n), (1, 0, cut)], "s": [(2, 0, n), (3, 0, n)] + ([(1, cut, n)] if cut < n else [])}
+        for q in "vs":
+            wait(q, *need)
+            for t, lo, hi in parts[q]:
+                copy(q, T["gt%d" % b][:, 4 * (c0 + lo) + t:4 * (c0 + hi):4],
+                     T.vt[:, t:2048].indirect(T.lst[:, l0 + lo // 16:l0 + hi // 16]), "ga%s%d" % (q, b))
+        wait("v", ("gav%d" % b, len(parts["v"])), ("gas%d" % b, len(parts["s"])))
+        if b == last:
+            wait("v", ("go", 4))
+            V.quantize_mx(T["k%d" % b][:, 64:nl + 192], T["ks%d" % b][:, 64:nl + 192], T["gt%d" % b][:, :]).then_inc(sem["q%d" % b], 1)
+        else:
+            V.quantize_mx(T["k%d" % b][:, :], T["ks%d" % b][:, :], T["gt%d" % b][:, :]).then_inc(sem["q%d" % b], 1)
 
+    wait("v", ("ld_s", 128))
+    V.tensor_scalar(T.s1i[:, :], T.sw[:, :], 128 * me, 640, A.is_lt, A.mult).then_inc(sem["sa"], 1)
     wait("v", ("ld_a", 16))
     V.quantize_mx(T.aq[:, :], T.aqs[:, :], T.at[:, :]).then_inc(sem["qa"], 1)
-    wait("v", ("ld_s", 128))
-    V.tensor_scalar(T.s1i[:, :], T.sw[:, :], 128 * me, 640, AluOpType.is_lt, AluOpType.mult).then_inc(sem["sa"], 1)
-    V.tensor_scalar(T.s2i[:, :], T.sw[:, :], 128 * me, None, AluOpType.subtract).then_inc(sem["sb"], 1)
-    wait("v", ("it3", 1))
-    V.tensor_scalar(T.idn[:, :], T.e3[:, :], 0.0, None, AluOpType.is_equal).then_inc(sem["idn"], 1)
-    wait("v", ("sa", 1), ("sb", 1))
-    V.tensor_tensor(T.s3i[:, :], T.s1i[:, :], T.s2i[:, :], AluOpType.add).then_inc(sem["sc"], 1)
-    wait("v", ("sc", 1))
-    V.tensor_copy(T.sl[:, :], T.s3i[:, :]).then_inc(sem["sl"], 1)
+    wait("v", ("sa", 1))
+    V.tensor_tensor(T.s2i[:, :], T.s1i[:, :], T.sw[:, :], A.add).then_inc(sem["sb"], 1)
+    wait("v", ("sb", 1))
+    V.tensor_scalar(T.sl[:, :], T.s2i[:, :], 128 * me, None, A.subtract).then_inc(sem["sl"], 1)
+    for k in range(4):
+        for o in range(2):
+            V.tensor_scalar(T.slx[:, 16 * k + 8 * o:16 * k + 8 * o + 8], T.s2i[:, 8 * k:8 * k + 8], 640 * o - 128 * me, None,
+                            A.add).then_inc(sem["sl"], 1)
 
-    bank0, bank2, bankt = (4, 0, 1, 2), (3, 4, 0, 1), (2, 3, 4)
+    def P(k, n, lo=0):
+        return T.ps[:, 512 * k + lo:512 * k + lo + n]
 
-    def P(k, n):
-        return T.pu[:, 512 * k:512 * k + n]
-
-    def E(b):
-        return T.eq[:, 128 * b:128 * b + 128], T.eqs[:, 128 * b:128 * b + 128]
-
+    order = (2, 0, 1, 3)
+    rounds = []
+    for b, ds in enumerate(BATCHES):
+        if b == last:
+            K, KS = T["k%d" % b], T["ks%d" % b]
+            rounds.append((NB, "arrn", 2 * nshare, K[:, pair:pair + 128], KS[:, pair:pair + 128], 0, 128))
+        rounds.append((b, "arr%d" % b, 2 * len(off_eng), T["r%d" % b][:, :], T["rs%d" % b][:, :], 128 * (nch - ds[-1]), 128 * len(ds)))
     PE.wait_ge(sem["eqd"], 1)
-    PE.wait_ge(sem["arr1"], 8 * share)
-    for b in range(4):
-        PE.matmul_mx(P(b, 256), *E(b), T.r1[:, :], T.r1s[:, :], True, True).then_inc(sem["mb1_%d" % b], 1)
-    PE.wait_ge(sem["q2"], 1)
-    PE.wait_ge(sem["arrn"], 2 * share)
-    for b in range(4):
-        if b:
-            PE.wait_ge(sem["cb1_%d" % (b - 1)], 1)
-        PE.matmul_mx(P(bank0[b], 128), *E(b), T.k2[:, pair:pair + 128], T.k2s[:, pair:pair + 128], True, True).then_inc(sem["mb0_%d" % b], 1)
-    PE.wait_ge(sem["arr2"], 8 * share)
-    for b in range(4):
-        PE.wait_ge(sem["cb1_3"] if b == 0 else sem["cb0_%d" % (b - 1)], 1)
-        PE.matmul_mx(P(bank2[b], 256), *E(b), T.r2[:, :], T.r2s[:, :], True, True).then_inc(sem["mb2_%d" % b], 1)
-    PE.wait_ge(sem["idn"], 1)
-    PE.wait_ge(sem["qa"], 1)
+    for i, (b, s, n, codes, plane, first, width) in enumerate(rounds):
+        if b == NB:
+            PE.wait_ge(sem["q%d" % last], 1)
+        PE.wait_ge(sem[s], n)
+        for o in order:
+            if i >= 2:
+                PE.wait_ge(sem["c%d_%d" % (rounds[i - 2][0], o)], 1)
+            PE.matmul_mx(P(4 * (i % 2) + o, width), T.eq[:, 128 * o:128 * o + 128], T.eqs[:, 128 * o:128 * o + 128], codes, plane,
+                         True, True).then_inc(sem["m%d_%d" % (b, o)], 1)
+    nr = len(rounds)
+    lo_, hi_ = 4 * (nr % 2), 4 * ((nr - 1) % 2)
+    ybank = {2: lo_ + 1, 0: lo_ + 2, 1: lo_ + 3, 3: lo_}
 
-    def product(o, k):
+    def free(i, os_):
+        for o in os_:
+            PE.wait_ge(sem["c%d_%d" % (rounds[i][0], o)], 1)
+
+    def product(o):
         PE.wait_ge(sem["hq%d" % o], 1)
-        PE.matmul_mx(T.py[:, 512 * k:512 * k + 256], T.hq[:, 128 * o:128 * o + 128], T.hqs[:, 128 * o:128 * o + 128],
+        PE.matmul_mx(P(ybank[o], 256), T.hq[:, 128 * o:128 * o + 128], T.hqs[:, 128 * o:128 * o + 128],
                      T.aq[:, :], T.aqs[:, :], True, True).then_inc(sem["ym%d" % o], 1)
 
-    for o in range(3):
-        PE.wait_ge(sem["gv%d" % o], 1)
-        PE.wait_ge(sem["gs%d" % o], 1)
-        PE.wait_ge(sem["cb0_3"] if o == 0 else sem["cb2_%d" % (o - 1)], 1)
-        for t in range(4):
-            PE.transpose(T.pu[:, 512 * bankt[o] + t:512 * bankt[o] + 512:4], T.gg[:, 512 * o + t:512 * o + 512:4], T.idn[:, :]).then_inc(sem["tr%d" % o], 1)
+    PE.wait_ge(sem["idn"], 1)
+    PE.wait_ge(sem["qa"], 1)
+    free(nr - 2, range(4))
+    PE.wait_ge(sem["gv2"], 1)
+    PE.wait_ge(sem["gs2"], 1)
+    for t in range(4):
+        PE.transpose(T.ps[:, 512 * lo_ + t:512 * lo_ + 512:4], T.gg[:, t:512:4], T.idn[:, :]).then_inc(sem["tr2"], 1)
+    free(nr - 1, range(4))
     PE.wait_ge(sem["gv3"], 1)
     PE.wait_ge(sem["gs3"], 1)
     for t in range(4):
-        PE.wait_ge(sem[("cb2_2", "cb2_3", "hc0", "hc1")[t]], 1)
-        PE.transpose(P(t, 128), T.gg[:, 1536 + t:2048:4], T.idn[:, :]).then_inc(sem["tt%d" % t], 1)
-        if t == 1:
-            product(0, 0)
-    product(1, 1)
-    product(2, 2)
-    PE.wait_ge(sem["yc0"], 1)
-    product(3, 0)
+        PE.transpose(P(hi_ + t, 128), T.gg[:, 512 + t:1024:4], T.idn[:, :]).then_inc(sem["tt%d" % t], 1)
+        if t == 2:
+            product(2)
+    product(0)
+    product(3)
+    product(1)
 
-    def towin(q, b):
-        for n, banks, first, width in (("b1_", (0, 1, 2, 3), 384, 256), ("b0_", bank0, 0, 128)):
-            pass
+    def unpacked(q, i, o):
+        b, _, _, _, _, first, width = rounds[i]
+        wait(q, ("m%d_%d" % (b, o), 1))
+        copy(q, T.w[:, 640 * o + first:640 * o + first + width], P(4 * (i % 2) + o, width), "c%d_%d" % (b, o))
 
-    def unpacked(q, n, b, bank, first, width):
-        wait(q, ("m%s%d" % (n, b), 1))
-        copy(q, T.w[:, 640 * b + first:640 * b + first + width], P(bank, width), "c%s%d" % (n, b))
+    def filled(q, o):
+        wait(q, *[("c%d_%d" % (r[0], o), 1) for r in rounds])
 
     def choose(q, o):
-        wait(q, ("sl", 1), ("cb1_%d" % o, 1), ("cb0_%d" % o, 1), ("cb2_%d" % o, 1))
+        filled(q, o)
         k = 0 if q == "v" else 1
-        copy(q, T.gg[:, 512 * o + 256 * k:512 * o + 256 * k + 256], T.w[:, 640 * o:640 * o + 640].indirect(T.sl[:, 16 * k:16 * k + 16]), "g%s%d" % (q, o))
+        copy(q, T.gg[:, 512 * (o - 2) + 256 * k:512 * (o - 2) + 256 * k + 256],
+             T.w[:, 640 * o:640 * o + 640].indirect(T.sl[:, 16 * k:16 * k + 16]), "g%s%d" % (q, o))
 
-    def block(q, o):
-        wait(q, ("tr%d" % o, 4))
-        copy(q, T.ht[:, 512 * o:512 * o + 512], P(bankt[o], 512), "hc%d" % o)
+    def quarter(q, k):
+        copy(q, T.gd[:, 256 * k:256 * k + 256], T.w[:, 0:1280].indirect(T.slx[:, 16 * k:16 * k + 16]), "gd%d" % k)
+
+    def squares(o):
+        for t in range(4):
+            V.transpose(T.ht[:, 512 * o + t:512 * o + 512:4], T.xd[:, 512 * o + t:512 * o + 512:4]).then_inc(sem["hc%d" % o], 1)
 
     def piece(q, t):
         wait(q, ("tt%d" % t, 1))
-        copy(q, T.ht[:, 1536 + t:2048:4], P(t, 128), "hp%d" % t)
+        copy(q, T.ht[:, 1536 + t:2048:4], P(hi_ + t, 128), "hp%d" % t)
+
+    made = {0: [("hc0", 4)], 1: [("hc1", 4)], 2: [("hc2", 1)], 3: [("hp%d" % t, 1) for t in range(4)]}
 
     def quant(o):
-        wait("v", *([("hc%d" % o, 1)] if o < 3 else [("hp%d" % t, 1) for t in range(4)]))
+        wait("v", *made[o])
         V.quantize_mx(T.hq[:, 128 * o:128 * o + 128], T.hqs[:, 128 * o:128 * o + 128], T.ht[:, 512 * o:512 * o + 512]).then_inc(sem["hq%d" % o], 1)
 
-    def result(q, o, k):
+    def result(q, o):
         wait(q, ("ym%d" % o, 1))
-        copy(q, T.yt[:, 256 * o:256 * o + 256], T.py[:, 512 * k:512 * k + 256], "yc%d" % o)
+        copy(q, T.yt[:, 256 * o:256 * o + 256], P(ybank[o], 256), "yc%d" % o)
 
-    for q, bs in (("v", (0, 2)), ("s", (1, 3))):
-        for b in bs:
-            unpacked(q, "b1_", b, b, 384, 256)
-        for b in bs:
-            unpacked(q, "b0_", b, bank0[b], 0, 128)
-        for o, b in ((0, bs[0]), (1, bs[1])):
-            unpacked(q, "b2_", b, bank2[b], 128, 256)
-            choose(q, o)
+    for q, os_, ks in (("v", (2, 1), (0, 1)), ("s", (0, 3), (2, 3))):
+        for i in range(nr - 1):
+            for o in os_:
+                unpacked(q, i, o)
+        unpacked(q, nr - 1, os_[0])
+        wait(q, ("sl", 9))
         choose(q, 2)
+        unpacked(q, nr - 1, os_[1])
+        filled(q, 0)
+        filled(q, 1)
+        for k in ks:
+            quarter(q, k)
         choose(q, 3)
-    block("v", 1)
-    block("s", 0)
-    quant(0)
-    quant(1)
-    block("s", 2)
+    wait("v", ("tr2", 4))
+    copy("v", T.ht[:, 1024:1536], P(lo_, 512), "hc2")
     quant(2)
-    piece("s", 0)
-    result("s", 0, 0)
-    piece("s", 2)
-    piece("v", 1)
-    piece("v", 3)
+    wait("v", ("xd", 64))
+    squares(0)
+    quant(0)
+    squares(1)
     quant(3)
-    result("v", 1, 1)
-    result("s", 2, 2)
-    result("v", 3, 0)
+    quant(1)
+    for t in range(4):
+        piece("s", t)
+    result("s", 2)
+    result("s", 0)
+    result("s", 3)
+    result("v", 1)
+
+    for k in (0, 2, 1, 3):
+        SY.wait_ge(sem["gd%d" % k], 1)
+        SY.dma_start(T.xd[32 * k:32 * k + 32, :], T.gd[:, 256 * k:256 * k + 256]).then_inc(sem["xd"], 16)
 
     def store_h(o):
-        for s in (["hc%d" % o] if o < 3 else ["hp%d" % t for t in range(4)]):
-            SY.wait_ge(sem[s], 1)
+        for s, n in made[o]:
+            SY.wait_ge(sem[s], n)
         SY.dma_start(T.h[:, 512 * o:512 * o + 512], T.ht[:, 512 * o:512 * o + 512]).then_inc(sem["stored"], 16)
 
     def store_y(o):
         SY.wait_ge(sem["yc%d" % o], 1)
         SY.dma_start(T.y[:, 256 * o:256 * o + 256], T.yt[:, 256 * o:256 * o + 256]).then_inc(sem["stored"], 16)
 
-    store_h(0)
-    store_h(1)
     store_h(2)
-    store_y(0)
+    store_h(0)
     store_h(3)
-    for o in (1, 2, 3):
+    store_y(2)
+    store_h(1)
+    for o in (0, 3, 1):
         store_y(o)
     SY.wait_ge(sem["stored"], 128)

@@ -2,19 +2,28 @@ from concourse.bass import DstId, RemoteDMATransfer
 from concourse.mybir import dt, AluOpType, ActivationFunctionType
 
 BF, F32, I32, U16, CODE, U8 = "bfloat16", "float32", "int32", "uint16", "float8_e4m3fn_x4", "uint8"
-BATCHES = ((1,), (2, 3), (4,))
-LISTS = ((1, 2), (3, 4))
-HELP = (0, 96, 64)
-NB = len(BATCHES)
+ORDER = [(1, 0), (1, 1), (2, 0), (2, 1), (3, 0), (0, 1), (3, 1), (4, 0), (4, 1)]
+LISTS = ((0, 1), (1, 3), (3, 6), (6, 8), (8, 9))
+BATCHES = ((0, 1), (1, 3), (3, 6), (6, 8), (8, 9))
+SENDS = ((0, 1), (1, 2), (2, 3), (3, 4), (4, 6), (6, 7), (7, 8), (8, 9))
+HELP = (0, 32, 96, 64, 64)
+HOLD = ()
+ROUNDS = ((1,), (2,), (0,), (3,), (4,))
+CUT = {2: 224, 3: 256}
+TAIL = {"tensor": "u2013 t20 t21 t22 t23 t30 t31 y2 t32 t33 y0 y1 y3 y4",
+        "v": "c0 c1 g2 k0 k1 g3 b2 q2 s0 q0 q3 y1 y4",
+        "s": "c2 g2 c3 k2 k3 g3 p0 p1 y2 p2 p3 y0 y3",
+        "sync": "x0 x2 x1 x3 h2 y2 h0 h3 y0 y1 y3"}
+EARLY = {"v": ((), (), (2, 0), (2, 0)), "s": ((2, 3, 0, 1), (2, 3, 0, 1), (3, 1), (3, 1))}
 SCRATCH = {
-    "wl": ("sbuf", [128, 40], I32),
+    "wl": ("sbuf", [64, 40], I32),
     "sw": ("sbuf", [128, 32], I32),
+    "slx": ("sbuf", [128, 64], U16),
     "loff": ("sbuf", [128, 40], U16),
     "lst": ("sbuf", [128, 40], U16),
     "s1i": ("sbuf", [128, 32], I32),
     "s2i": ("sbuf", [128, 32], I32),
     "sl": ("sbuf", [128, 32], U16),
-    "slx": ("sbuf", [128, 64], U16),
     "vt": ("sbuf", [128, 2048], BF),
     "at": ("sbuf", [128, 1024], BF),
     "ea": ("sbuf", [128, 128], BF), "eb": ("sbuf", [128, 128], BF), "ec": ("sbuf", [128, 2], BF),
@@ -23,29 +32,24 @@ SCRATCH = {
     "eq": ("sbuf", [128, 512], CODE), "eqs": ("sbuf", [128, 512], U8),
     "aq": ("sbuf", [128, 256], CODE), "aqs": ("sbuf", [128, 256], U8),
     "hq": ("sbuf", [128, 512], CODE), "hqs": ("sbuf", [128, 512], U8),
+    "gt": ("sbuf", [128, 4 * 1024], BF),
+    "k": ("sbuf", [128, 1024], CODE), "ks": ("sbuf", [128, 1024], U8),
+    "r": ("sbuf", [128, 512], CODE), "rs": ("sbuf", [128, 512], U8),
     "w": ("sbuf", [128, 2560], BF),
-    "gg": ("sbuf", [128, 1024], F32),
+    "g2": ("sbuf", [128, 512], F32), "g3": ("sbuf", [128, 512], F32),
     "gd": ("sbuf", [128, 1024], BF),
     "xd": ("sbuf", [128, 1024], BF),
     "ht": ("sbuf", [128, 2048], BF),
     "yt": ("sbuf", [128, 1024], F32),
     "ps": ("psum", [128, 4096], F32),
 }
-for _b, _ds in enumerate(BATCHES):
-    _n = 128 * len(_ds)
-    _x = 128 if _b == NB - 1 else 0
-    SCRATCH["gt%d" % _b] = ("sbuf", [128, 4 * (_n + _x)], BF)
-    SCRATCH["k%d" % _b] = ("sbuf", [128, _n + 2 * _x], CODE)
-    SCRATCH["ks%d" % _b] = ("sbuf", [128, _n + 2 * _x], U8)
-    SCRATCH["r%d" % _b] = ("sbuf", [128, _n], CODE)
-    SCRATCH["rs%d" % _b] = ("sbuf", [128, _n], U8)
 SEMAPHORES = (["ld_w", "ld_v", "ld_a", "ld_s", "ita", "itb", "itc", "cv", "eb", "eqd", "go", "qa", "sa", "sb", "sl", "idn",
-               "arrn", "sent", "stored", "xd"]
+               "sent", "stored", "tr2", "xd", "gz", "ym4", "yc4"]
               + ["l%d" % i for i in range(len(LISTS))]
-              + ["%s%d" % (n, b) for n in ("gav", "gas", "q", "arr") for b in range(NB)]
-              + ["%s%d_%d" % (n, b, o) for n in ("m", "c") for b in range(NB + 1) for o in range(4)]
-              + ["%s%d" % (n, b) for n in ("gd", "tt", "hp", "hc", "hq", "ym", "yc") for b in range(4)]
-              + ["gv2", "gs2", "gv3", "gs3", "tr2"])
+              + ["%s%d" % (n, b) for n in ("gav", "gas", "q") for b in range(len(BATCHES))]
+              + ["arr%d" % d for d in range(5)]
+              + ["%s%d_%d" % (n, b, o) for n in ("m", "c") for b in range(len(ROUNDS)) for o in range(4)]
+              + ["%s%d" % (n, b) for n in ("gv", "gs", "gd", "tt", "hp", "hc", "hq", "ym", "yc") for b in range(4)])
 
 
 def rank_program(g, core, T, topo):
@@ -65,69 +69,67 @@ def rank_program(g, core, T, topo):
     me = chips.index(topo.chip(core))
     par = members[me].index(rank)
     nbr = members[me][1 - par]
-    last = NB - 1
 
     def at(d):
         return members[(me + d) % nch]
 
-    for q, lo in ((SY, 0), (S, 4)):
-        for k in range(lo, lo + 4):
-            q.dma_start(T.wl[16 * k:16 * k + 16, :], T.want[:, :]).then_inc(sem["ld_w"], 16)
+    dests = [at(d)[par ^ e] for d, e in ORDER]
+    servers = [at(-d)[par ^ e] for d, e in ORDER]
+    first, own, pair = (0, 64, 64) if par == 0 else (128, 64, 0)
+    kcol, zeros, x = [first], [], 192
+    for lo, hi in BATCHES[1:]:
+        kcol += [x + 64 * i for i in range(hi - lo)]
+        x += 64 * (hi - lo)
+        if hi - lo == 1:
+            zeros.append(x)
+            x += 64
+
+    for k in range(4):
+        (SY, S)[k % 2].dma_start(T.wl[16 * k:16 * k + 16, :], T.want[:, :]).then_inc(sem["ld_w"], 16)
     SY.dma_start(T.vt[:, :], T.v[:, :]).then_inc(sem["ld_v"], 16)
+    for k in range(8):
+        (S, SY)[k % 2].dma_start(T.sw[16 * k:16 * k + 16, :], T.slot[:, :]).then_inc(sem["ld_s"], 16)
     SY.dma_start(T.at[:, :], T.a[:, :]).then_inc(sem["ld_a"], 16)
-    for q, lo in ((SY, 0), (S, 4)):
-        for k in range(lo, lo + 4):
-            q.dma_start(T.sw[16 * k:16 * k + 16, :], T.slot[:, :]).then_inc(sem["ld_s"], 16)
 
     g.iota(T.ec[:, :], [[0, 2]], 0, 4, allow_small_or_imprecise_dtypes=True).then_inc(sem["itc"], 1)
     g.iota(T.ea[:, :], [[1, 128]], 0, 0, allow_small_or_imprecise_dtypes=True).then_inc(sem["ita"], 1)
     g.iota(T.eb[:, :], [[1, 32], [64, 4]], 0, 0, allow_small_or_imprecise_dtypes=True).then_inc(sem["itb"], 1)
 
     off_eng = topo.engines(core, T.cores[at(1)[0]])
-    spare = [e for e in topo.engines(core, T.cores[nbr]) if e not in off_eng][::2]
-
-    def share(ds):
-        return len(off_eng) // (2 * len(ds))
-
-    nshare = min(share(BATCHES[last]), len(spare))
+    spare = [e for e in topo.engines(core, T.cores[nbr]) if e not in off_eng][::2][:2]
     sent = [0]
 
-    def send(ds, items, to_nbr=None):
-        n = share(ds)
-        sets = [off_eng[n * m:n * m + n] for m in range(len(items))]
-        if to_nbr:
-            items, sets = items + [to_nbr], sets + [spare[:nshare]]
+    def engines(lo, hi, thin=False):
+        far = [i for i in range(lo, hi) if ORDER[i][0]]
+        eng = off_eng[::2] if thin else off_eng
+        n = len(eng) // max(len(far), 1)
+        return {i: eng[n * far.index(i):n * far.index(i) + n] if i in far else spare for i in range(lo, hi)}
+
+    def send(lo, hi, item, thin=False):
         trs = []
-        for (r, s, d, x), es in zip(items, sets):
+        for i, es in engines(lo, hi, thin).items():
+            r, s, d, x = item(i)
             rid, pid, _ = topo.addr(T.cores[r])
             trs.append(RemoteDMATransfer(dst_ids=[DstId(rid=rid, pnc=pid)], dma_engine_mask=sum(1 << e for e in es),
                                          remote_sem=sem[s], srcs=[x], dsts=[d], alu_op=0))
             sent[0] += len(es)
         g.remote_dma_fused(trs, local_sem=sem["sent"])
 
-    g.wait_ge(sem["cv"], 1)
-    for i, ds in enumerate(LISTS):
-        s = "l%d" % i
-        send(ds, [(r, s, T.lst[:, 8 * d - 8 + 4 * par:8 * d - 4 + 4 * par], T.loff[:, 4 * r:4 * r + 4]) for d in ds for r in at(-d)],
-             (nbr, s, T.lst[:, 32:36], T.loff[:, 4 * nbr:4 * nbr + 4]) if i == len(LISTS) - 1 else None)
-    lcount = [len(off_eng) + (nshare if i == len(LISTS) - 1 else 0) for i in range(len(LISTS))]
+    g.wait_ge(sem["cv"], 2)
+    for k, (lo, hi) in enumerate(LISTS):
+        send(lo, hi, lambda i: (servers[i], "l%d" % k, T.lst[:, 4 * i:4 * i + 4], T.loff[:, 4 * servers[i]:4 * servers[i] + 4]), k == 0)
 
-    nl = 128 * len(BATCHES[last])
-    base = 64 + 64 * par
-    pair = nl + 128 if par == 0 else 0
-    nland = nl + 192 if par == 1 else 0
-    for b, ds in enumerate(BATCHES):
-        x0 = base if b == last else 0
-        to = [(r, 128 * (len(ds) - 1 - i) + 64 * par, x0 + 128 * i + 64 * j) for i, d in enumerate(ds) for j, r in enumerate(at(d))]
-        g.wait_ge(sem["q%d" % b], 1)
-        for k, r_, cast in (("k", "r", True), ("ks", "rs", False)):
-            K, R_ = T["%s%d" % (k, b)], T["%s%d" % (r_, b)]
-
-            def view(buf, c):
-                return buf[:, c:c + 64].bitcast(dt.uint8) if cast else buf[:, c:c + 64]
-            send(ds, [(r, "arr%d" % b, view(R_, d), view(K, x)) for r, d, x in to],
-                 (nbr, "arrn", view(K, nland), view(K, base + nl)) if b == last else None)
+    for lo, hi in SENDS:
+        for b, (x, z) in enumerate(BATCHES):
+            if x <= lo < z:
+                g.wait_ge(sem["q%d" % b], 1)
+        for K, R_, view in ((T.k, T.r, lambda buf, c: buf[:, c:c + 64].bitcast(dt.uint8)), (T.ks, T.rs, lambda buf, c: buf[:, c:c + 64])):
+            send(lo, hi, lambda i: (dests[i], "arr%d" % ORDER[i][0],
+                                    view(R_, 128 * (nch - 1 - ORDER[i][0]) + 64 * par) if ORDER[i][0] else view(K, 128 * par), view(K, kcol[i])))
     g.wait_ge(sem["sent"], sent[0])
+
+    def arrived(d):
+        return sum(2 * len(es) for lo, hi in SENDS for i, es in engines(lo, hi).items() if ORDER[i][0] == d)
 
     def copy(q, out, in_, s):
         if q == "v":
@@ -144,189 +146,169 @@ def rank_program(g, core, T, topo):
             V.tensor_scalar(T.idt[:, 512 * o + t:512 * o + 512:4], (T.eb if o < 2 else T.ea)[:, :], float((32 if o < 2 else 128) * o - t),
                             T.ec[:, 0:1], A.add, A.is_equal).then_inc(sem["eb"], 1)
 
-    wait("v", ("itc", 1), ("ita", 1))
+    for x in zeros:
+        V.memset(T.gt[:, 4 * x:4 * x + 256], 0.0).then_inc(sem["gz"], 1)
+    wait("v", ("gz", len(zeros)), ("itc", 1), ("ita", 1))
+    wait("v", ("ld_w", 64))
+    for hf in range(2):
+        V.tensor_scalar(T.loff[64 * hf:64 * hf + 64, :], T.wl[:, :], 0, 4, A.max, A.mult).then_inc(sem["cv"], 1)
     ones(2)
-    wait("v", ("ld_w", 128))
-    V.tensor_scalar(T.loff[:, :], T.wl[:, :], 0, 4, A.max, A.mult).then_inc(sem["cv"], 1)
     ones(3)
     wait("v", ("itb", 1))
     ones(0)
     ones(1)
-    V.tensor_scalar(T.idn[:, :], T.ea[:, :], 4.0, T.ec[:, 0:1], A.mult, A.is_equal).then_inc(sem["idn"], 1)
-    wait("v", ("eb", 16))
-    V.quantize_mx(T.eq[:, :], T.eqs[:, :], T.idt[:, :]).then_inc(sem["eqd"], 1)
-
-    goff = 64 * par
-    gown = nl + 64 if par == 0 else 0
-    wait("s", ("ld_v", 16), ("cv", 1))
-    for t in range(4):
-        copy("s", T["gt%d" % last][:, 4 * gown + t:4 * gown + 256:4], T.vt[:, t:2048].indirect(T.loff[:, 4 * rank:4 * rank + 4]), "go")
-    wait("v", ("ld_v", 16))
-    for b, ds in enumerate(BATCHES):
-        n = 128 * len(ds) + (64 if b == last else 0)
-        c0 = goff if b == last else 0
-        l0 = 8 * ds[0] - 8
-        need = [("l%d" % i, lcount[i]) for i, ls in enumerate(LISTS) if set(ls) & set(ds) or (b == last and i == len(LISTS) - 1)]
-        cut = n - HELP[b]
-        parts = {"v": [(0, 0, n), (1, 0, cut)], "s": [(2, 0, n), (3, 0, n)] + ([(1, cut, n)] if cut < n else [])}
-        for q in "vs":
-            wait(q, *need)
-            for t, lo, hi in parts[q]:
-                copy(q, T["gt%d" % b][:, 4 * (c0 + lo) + t:4 * (c0 + hi):4],
-                     T.vt[:, t:2048].indirect(T.lst[:, l0 + lo // 16:l0 + hi // 16]), "ga%s%d" % (q, b))
-        wait("v", ("gav%d" % b, len(parts["v"])), ("gas%d" % b, len(parts["s"])))
-        if b == last:
-            wait("v", ("go", 4))
-            V.quantize_mx(T["k%d" % b][:, 64:nl + 192], T["ks%d" % b][:, 64:nl + 192], T["gt%d" % b][:, :]).then_inc(sem["q%d" % b], 1)
-        else:
-            V.quantize_mx(T["k%d" % b][:, :], T["ks%d" % b][:, :], T["gt%d" % b][:, :]).then_inc(sem["q%d" % b], 1)
-
     wait("v", ("ld_s", 128))
     V.tensor_scalar(T.s1i[:, :], T.sw[:, :], 128 * me, 640, A.is_lt, A.mult).then_inc(sem["sa"], 1)
-    wait("v", ("ld_a", 16))
-    V.quantize_mx(T.aq[:, :], T.aqs[:, :], T.at[:, :]).then_inc(sem["qa"], 1)
+    wait("v", ("eb", 16))
+    V.quantize_mx(T.eq[:, :], T.eqs[:, :], T.idt[:, :]).then_inc(sem["eqd"], 1)
     wait("v", ("sa", 1))
     V.tensor_tensor(T.s2i[:, :], T.s1i[:, :], T.sw[:, :], A.add).then_inc(sem["sb"], 1)
+
+    wait("s", ("ld_v", 16), ("cv", 2))
+    for t in range(4):
+        copy("s", T.gt[:, 4 * own + t:4 * own + 256:4], T.vt[:, t:2048].indirect(T.loff[:, 4 * rank:4 * rank + 4]), "go")
+    wait("v", ("ld_v", 16), ("go", 4))
+
+    def codes(b, c0, n, nv, ns):
+        wait("v", ("gav%d" % b, nv), ("gas%d" % b, ns))
+        V.quantize_mx(T.k[:, c0:c0 + n], T.ks[:, c0:c0 + n], T.gt[:, 4 * c0:4 * (c0 + n)]).then_inc(sem["q%d" % b], 1)
+
+    held = []
+    for b, (lo, hi) in enumerate(BATCHES):
+        c0, n = kcol[lo], 64 * (hi - lo)
+        cut = n - HELP[b]
+        parts = {"v": [(0, 0, n)] + ([(1, 0, cut)] if cut else []), "s": [(2, 0, n), (3, 0, n)] + ([(1, cut, n)] if cut < n else [])}
+        for q in "vs":
+            wait(q, *[("l%d" % k, sum(len(es) for es in engines(x, z, k == 0).values())) for k, (x, z) in enumerate(LISTS) if x < hi and lo < z])
+            for t, x, z in parts[q]:
+                copy(q, T.gt[:, 4 * (c0 + x) + t:4 * (c0 + z):4], T.vt[:, t:2048].indirect(T.lst[:, 4 * lo + x // 16:4 * lo + z // 16]),
+                     "ga%s%d" % (q, b))
+                if q == "v" and held:
+                    codes(*held.pop())
+        held.append((b, c0 if b else min(first, own), max(n, 128), len(parts["v"]), len(parts["s"])))
+        if b not in HOLD:
+            codes(*held.pop())
+
     wait("v", ("sb", 1))
     V.tensor_scalar(T.sl[:, :], T.s2i[:, :], 128 * me, None, A.subtract).then_inc(sem["sl"], 1)
     for k in range(4):
         for o in range(2):
             V.tensor_scalar(T.slx[:, 16 * k + 8 * o:16 * k + 8 * o + 8], T.s2i[:, 8 * k:8 * k + 8], 640 * o - 128 * me, None,
                             A.add).then_inc(sem["sl"], 1)
+    V.tensor_scalar(T.idn[:, :], T.ea[:, :], 4.0, T.ec[:, 0:1], A.mult, A.is_equal).then_inc(sem["idn"], 1)
+    wait("v", ("ld_a", 16))
+    V.quantize_mx(T.aq[:, :], T.aqs[:, :], T.at[:, :]).then_inc(sem["qa"], 1)
 
-    def P(k, n, lo=0):
-        return T.ps[:, 512 * k + lo:512 * k + lo + n]
+    def P(k, n):
+        return T.ps[:, 512 * k:512 * k + n]
 
-    order = (2, 0, 1, 3)
-    rounds = []
-    for b, ds in enumerate(BATCHES):
-        if b == last:
-            K, KS = T["k%d" % b], T["ks%d" % b]
-            rounds.append((NB, "arrn", 2 * nshare, K[:, pair:pair + 128], KS[:, pair:pair + 128], 0, 128))
-        rounds.append((b, "arr%d" % b, 2 * len(off_eng), T["r%d" % b][:, :], T["rs%d" % b][:, :], 128 * (nch - ds[-1]), 128 * len(ds)))
-    PE.wait_ge(sem["eqd"], 1)
-    for i, (b, s, n, codes, plane, first, width) in enumerate(rounds):
-        if b == NB:
-            PE.wait_ge(sem["q%d" % last], 1)
-        PE.wait_ge(sem[s], n)
-        for o in order:
-            if i >= 2:
-                PE.wait_ge(sem["c%d_%d" % (rounds[i - 2][0], o)], 1)
-            PE.matmul_mx(P(4 * (i % 2) + o, width), T.eq[:, 128 * o:128 * o + 128], T.eqs[:, 128 * o:128 * o + 128], codes, plane,
-                         True, True).then_inc(sem["m%d_%d" % (b, o)], 1)
-    nr = len(rounds)
-    lo_, hi_ = 4 * (nr % 2), 4 * ((nr - 1) % 2)
-    ybank = {2: lo_ + 1, 0: lo_ + 2, 1: lo_ + 3, 3: lo_}
+    nr = len(ROUNDS)
+    hi_, lo_ = 4 * ((nr - 1) % 2), 4 * (nr % 2)
+    results = {0: (lo_ + 1, "c%d_1" % (nr - 2), 0, 0, 256), 1: (lo_ + 3, "c%d_3" % (nr - 2), 1, 0, 256),
+               2: (lo_ + 2, "c%d_2" % (nr - 2), 2, 0, 256), 3: (lo_, "hc2", 3, 0, 128), 4: (hi_, "hp0", 3, 128, 128)}
 
-    def free(i, os_):
+    def unpack(i, *os_):
+        ds = ROUNDS[i]
+        for d in ds:
+            PE.wait_ge(sem["arr%d" % d], arrived(d))
+        x, n = 128 * (nch - 1 - ds[-1]), 128 * len(ds)
+        codes, plane = (T.r[:, x:x + n], T.rs[:, x:x + n]) if ds[0] else (T.k[:, pair:pair + 128], T.ks[:, pair:pair + 128])
         for o in os_:
-            PE.wait_ge(sem["c%d_%d" % (rounds[i][0], o)], 1)
+            if i >= 2:
+                PE.wait_ge(sem["c%d_%d" % (i - 2, o)], 1)
+            PE.matmul_mx(P(4 * (i % 2) + o, n), T.eq[:, 128 * o:128 * o + 128], T.eqs[:, 128 * o:128 * o + 128], codes, plane,
+                         True, True).then_inc(sem["m%d_%d" % (i, o)], 1)
 
-    def product(o):
-        PE.wait_ge(sem["hq%d" % o], 1)
-        PE.matmul_mx(P(ybank[o], 256), T.hq[:, 128 * o:128 * o + 128], T.hqs[:, 128 * o:128 * o + 128],
-                     T.aq[:, :], T.aqs[:, :], True, True).then_inc(sem["ym%d" % o], 1)
+    def product(i):
+        bank, free, o, x, n = results[i]
+        PE.wait_ge(sem[free], 1)
+        PE.wait_ge(sem["hq%d" % (o if o > 1 else 0)], 1)
+        PE.matmul_mx(P(bank, n), T.hq[:, 128 * o:128 * o + 128], T.hqs[:, 128 * o:128 * o + 128],
+                     T.aq[:, x:x + n], T.aqs[:, x:x + n], True, True).then_inc(sem["ym%d" % i], 1)
 
+    def turn(o, t):
+        if t == 0:
+            PE.wait_ge(sem["gv%d" % o], 1)
+            PE.wait_ge(sem["gs%d" % o], 1)
+        if o == 2:
+            PE.wait_ge(sem["c%d_0" % (nr - 2)], 1)
+            PE.transpose(T.ps[:, 512 * lo_ + t:512 * lo_ + 512:4], T.g2[:, t:512:4], T.idn[:, :]).then_inc(sem["tr2"], 1)
+        else:
+            PE.wait_ge(sem["c%d_%d" % (nr - 1, t)], 1)
+            PE.transpose(P(hi_ + t, 128), T.g3[:, t:512:4], T.idn[:, :]).then_inc(sem["tt%d" % t], 1)
+
+    PE.wait_ge(sem["eqd"], 1)
+    PE.wait_ge(sem["q0"], 1)
+    for i in range(nr - 1):
+        unpack(i, 2, 3, 0, 1)
     PE.wait_ge(sem["idn"], 1)
     PE.wait_ge(sem["qa"], 1)
-    free(nr - 2, range(4))
-    PE.wait_ge(sem["gv2"], 1)
-    PE.wait_ge(sem["gs2"], 1)
-    for t in range(4):
-        PE.transpose(T.ps[:, 512 * lo_ + t:512 * lo_ + 512:4], T.gg[:, t:512:4], T.idn[:, :]).then_inc(sem["tr2"], 1)
-    free(nr - 1, range(4))
-    PE.wait_ge(sem["gv3"], 1)
-    PE.wait_ge(sem["gs3"], 1)
-    for t in range(4):
-        PE.transpose(P(hi_ + t, 128), T.gg[:, 512 + t:1024:4], T.idn[:, :]).then_inc(sem["tt%d" % t], 1)
-        if t == 2:
-            product(2)
-    product(0)
-    product(3)
-    product(1)
+    for step in TAIL["tensor"].split():
+        n = [int(x) for x in step[1:]]
+        {"u": lambda *os_: unpack(nr - 1, *os_), "t": turn, "y": product}[step[0]](*n)
 
-    def unpacked(q, i, o):
-        b, _, _, _, _, first, width = rounds[i]
-        wait(q, ("m%d_%d" % (b, o), 1))
-        copy(q, T.w[:, 640 * o + first:640 * o + first + width], P(4 * (i % 2) + o, width), "c%d_%d" % (b, o))
-
-    def filled(q, o):
-        wait(q, *[("c%d_%d" % (r[0], o), 1) for r in rounds])
+    def unpacked(q, o, i=nr - 1):
+        ds = ROUNDS[i]
+        x, n = 640 * o + 128 * ((nch - ds[-1]) % nch), 128 * len(ds)
+        wait(q, ("m%d_%d" % (i, o), 1))
+        copy(q, T.w[:, x:x + n], P(4 * (i % 2) + o, n), "c%d_%d" % (i, o))
 
     def choose(q, o):
-        filled(q, o)
-        k = 0 if q == "v" else 1
-        copy(q, T.gg[:, 512 * (o - 2) + 256 * k:512 * (o - 2) + 256 * k + 256],
-             T.w[:, 640 * o:640 * o + 640].indirect(T.sl[:, 16 * k:16 * k + 16]), "g%s%d" % (q, o))
+        wait(q, ("sl", 9), *[("c%d_%d" % (i, o), 1) for i in range(nr)])
+        x, z = (0, CUT[o]) if q == "v" else (CUT[o], 512)
+        copy(q, T["g%d" % o][:, x:z], T.w[:, 640 * o:640 * o + 640].indirect(T.sl[:, x // 16:z // 16]), "g%s%d" % (q, o))
 
     def quarter(q, k):
+        wait(q, ("sl", 9), *[("c%d_%d" % (i, o), 1) for i in range(nr) for o in (0, 1)])
         copy(q, T.gd[:, 256 * k:256 * k + 256], T.w[:, 0:1280].indirect(T.slx[:, 16 * k:16 * k + 16]), "gd%d" % k)
 
-    def squares(o):
+    def squares(q, o):
+        wait("v", ("xd", 64))
         for t in range(4):
-            V.transpose(T.ht[:, 512 * o + t:512 * o + 512:4], T.xd[:, 512 * o + t:512 * o + 512:4]).then_inc(sem["hc%d" % o], 1)
+            V.transpose(T.ht[:, t:1024:4], T.xd[:, t:1024:4]).then_inc(sem["hc0"], 1)
+
+    def block(q, o):
+        wait(q, ("tr2", 4))
+        copy(q, T.ht[:, 1024:1536], P(lo_, 512), "hc2")
 
     def piece(q, t):
         wait(q, ("tt%d" % t, 1))
         copy(q, T.ht[:, 1536 + t:2048:4], P(hi_ + t, 128), "hp%d" % t)
 
-    made = {0: [("hc0", 4)], 1: [("hc1", 4)], 2: [("hc2", 1)], 3: [("hp%d" % t, 1) for t in range(4)]}
+    made = {0: [("hc0", 4)], 2: [("hc2", 1)], 3: [("hp%d" % t, 1) for t in range(4)]}
+    end = {0: 2, 2: 3, 3: 4}
 
-    def quant(o):
+    def quant(q, o):
         wait("v", *made[o])
-        V.quantize_mx(T.hq[:, 128 * o:128 * o + 128], T.hqs[:, 128 * o:128 * o + 128], T.ht[:, 512 * o:512 * o + 512]).then_inc(sem["hq%d" % o], 1)
+        V.quantize_mx(T.hq[:, 128 * o:128 * end[o]], T.hqs[:, 128 * o:128 * end[o]], T.ht[:, 512 * o:512 * end[o]]).then_inc(sem["hq%d" % o], 1)
 
-    def result(q, o):
-        wait(q, ("ym%d" % o, 1))
-        copy(q, T.yt[:, 256 * o:256 * o + 256], P(ybank[o], 256), "yc%d" % o)
+    def result(q, i):
+        bank, _, o, x, n = results[i]
+        wait(q, ("ym%d" % i, 1))
+        copy(q, T.yt[:, 256 * o + x:256 * o + x + n], P(bank, n), "yc%d" % i)
 
-    for q, os_, ks in (("v", (2, 1), (0, 1)), ("s", (0, 3), (2, 3))):
+    for q in "vs":
         for i in range(nr - 1):
-            for o in os_:
-                unpacked(q, i, o)
-        unpacked(q, nr - 1, os_[0])
-        wait(q, ("sl", 9))
-        choose(q, 2)
-        unpacked(q, nr - 1, os_[1])
-        filled(q, 0)
-        filled(q, 1)
-        for k in ks:
-            quarter(q, k)
-        choose(q, 3)
-    wait("v", ("tr2", 4))
-    copy("v", T.ht[:, 1024:1536], P(lo_, 512), "hc2")
-    quant(2)
-    wait("v", ("xd", 64))
-    squares(0)
-    quant(0)
-    squares(1)
-    quant(3)
-    quant(1)
-    for t in range(4):
-        piece("s", t)
-    result("s", 2)
-    result("s", 0)
-    result("s", 3)
-    result("v", 1)
+            for o in EARLY[q][i]:
+                unpacked(q, o, i)
+        for step in TAIL[q].split():
+            {"c": unpacked, "g": choose, "k": quarter, "s": squares, "b": block, "p": piece, "q": quant, "y": result}[step[0]](q, int(step[1]))
 
-    for k in (0, 2, 1, 3):
+    def exchange(k):
         SY.wait_ge(sem["gd%d" % k], 1)
         SY.dma_start(T.xd[32 * k:32 * k + 32, :], T.gd[:, 256 * k:256 * k + 256]).then_inc(sem["xd"], 16)
 
     def store_h(o):
         for s, n in made[o]:
             SY.wait_ge(sem[s], n)
-        SY.dma_start(T.h[:, 512 * o:512 * o + 512], T.ht[:, 512 * o:512 * o + 512]).then_inc(sem["stored"], 16)
+        SY.dma_start(T.h[:, 512 * o:512 * end[o]], T.ht[:, 512 * o:512 * end[o]]).then_inc(sem["stored"], 16)
 
     def store_y(o):
-        SY.wait_ge(sem["yc%d" % o], 1)
+        for i in results:
+            if results[i][2] == o:
+                SY.wait_ge(sem["yc%d" % i], 1)
         SY.dma_start(T.y[:, 256 * o:256 * o + 256], T.yt[:, 256 * o:256 * o + 256]).then_inc(sem["stored"], 16)
 
-    store_h(2)
-    store_h(0)
-    store_h(3)
-    store_y(2)
-    store_h(1)
-    for o in (0, 3, 1):
-        store_y(o)
-    SY.wait_ge(sem["stored"], 128)
+    for step in TAIL["sync"].split():
+        {"x": exchange, "h": store_h, "y": store_y}[step[0]](int(step[1]))
+    SY.wait_ge(sem["stored"], 112)

from concourse.bass import DstId, RemoteDMATransfer
from concourse.mybir import dt, AluOpType, ActivationFunctionType

BF, F32, I32, U16, CODE, U8 = "bfloat16", "float32", "int32", "uint16", "float8_e4m3fn_x4", "uint8"
ORDER = [(1, 0), (1, 1), (2, 0), (2, 1), (3, 0), (0, 1), (3, 1), (4, 0), (4, 1)]
LISTS = ((0, 1), (1, 3), (3, 6), (6, 8), (8, 9))
BATCHES = ((0, 1), (1, 3), (3, 6), (6, 8), (8, 9))
SENDS = ((0, 1), (1, 2), (2, 3), (3, 4), (4, 6), (6, 7), (7, 8), (8, 9))
HELP = (0, 32, 96, 64, 64)
HOLD = ()
ROUNDS = ((1,), (2,), (0,), (3,), (4,))
CUT = {2: 224, 3: 256}
TAIL = {"tensor": "u2013 t20 t21 t22 t23 t30 t31 y2 t32 t33 y0 y1 y3 y4",
        "v": "c0 c1 g2 k0 k1 g3 b2 q2 s0 q0 q3 y1 y4",
        "s": "c2 g2 c3 k2 k3 g3 p0 p1 y2 p2 p3 y0 y3",
        "sync": "x0 x2 x1 x3 h2 y2 h0 h3 y0 y1 y3"}
EARLY = {"v": ((), (), (2, 0), (2, 0)), "s": ((2, 3, 0, 1), (2, 3, 0, 1), (3, 1), (3, 1))}
SCRATCH = {
    "wl": ("sbuf", [64, 40], I32),
    "sw": ("sbuf", [128, 32], I32),
    "slx": ("sbuf", [128, 64], U16),
    "loff": ("sbuf", [128, 40], U16),
    "lst": ("sbuf", [128, 40], U16),
    "s1i": ("sbuf", [128, 32], I32),
    "s2i": ("sbuf", [128, 32], I32),
    "sl": ("sbuf", [128, 32], U16),
    "vt": ("sbuf", [128, 2048], BF),
    "at": ("sbuf", [128, 1024], BF),
    "ea": ("sbuf", [128, 128], BF), "eb": ("sbuf", [128, 128], BF), "ec": ("sbuf", [128, 2], BF),
    "idt": ("sbuf", [128, 2048], BF),
    "idn": ("sbuf", [128, 128], F32),
    "eq": ("sbuf", [128, 512], CODE), "eqs": ("sbuf", [128, 512], U8),
    "aq": ("sbuf", [128, 256], CODE), "aqs": ("sbuf", [128, 256], U8),
    "hq": ("sbuf", [128, 512], CODE), "hqs": ("sbuf", [128, 512], U8),
    "gt": ("sbuf", [128, 4 * 1024], BF),
    "k": ("sbuf", [128, 1024], CODE), "ks": ("sbuf", [128, 1024], U8),
    "r": ("sbuf", [128, 512], CODE), "rs": ("sbuf", [128, 512], U8),
    "w": ("sbuf", [128, 2560], BF),
    "g2": ("sbuf", [128, 512], F32), "g3": ("sbuf", [128, 512], F32),
    "gd": ("sbuf", [128, 1024], BF),
    "xd": ("sbuf", [128, 1024], BF),
    "ht": ("sbuf", [128, 2048], BF),
    "yt": ("sbuf", [128, 1024], F32),
    "ps": ("psum", [128, 4096], F32),
}
SEMAPHORES = (["ld_w", "ld_v", "ld_a", "ld_s", "ita", "itb", "itc", "cv", "eb", "eqd", "go", "qa", "sa", "sb", "sl", "idn",
               "sent", "stored", "tr2", "xd", "gz", "ym4", "yc4"]
              + ["l%d" % i for i in range(len(LISTS))]
              + ["%s%d" % (n, b) for n in ("gav", "gas", "q") for b in range(len(BATCHES))]
              + ["arr%d" % d for d in range(5)]
              + ["%s%d_%d" % (n, b, o) for n in ("m", "c") for b in range(len(ROUNDS)) for o in range(4)]
              + ["%s%d" % (n, b) for n in ("gv", "gs", "gd", "tt", "hp", "hc", "hq", "ym", "yc") for b in range(4)])


def rank_program(g, core, T, topo):
    rank = T.rank_of(core)
    if rank is None:
        return
    V, S, PE, SY = g.vector, g.scalar, g.tensor, g.sync
    sem = T.sem
    A = AluOpType
    COPY = ActivationFunctionType.Copy
    chips = []
    for c in T.cores:
        if topo.chip(c) not in chips:
            chips.append(topo.chip(c))
    members = [[T.rank_of(c) for c in T.cores if topo.chip(c) == ch] for ch in chips]
    nch = len(chips)
    me = chips.index(topo.chip(core))
    par = members[me].index(rank)
    nbr = members[me][1 - par]

    def at(d):
        return members[(me + d) % nch]

    dests = [at(d)[par ^ e] for d, e in ORDER]
    servers = [at(-d)[par ^ e] for d, e in ORDER]
    first, own, pair = (0, 64, 64) if par == 0 else (128, 64, 0)
    kcol, zeros, x = [first], [], 192
    for lo, hi in BATCHES[1:]:
        kcol += [x + 64 * i for i in range(hi - lo)]
        x += 64 * (hi - lo)
        if hi - lo == 1:
            zeros.append(x)
            x += 64

    for k in range(4):
        (SY, S)[k % 2].dma_start(T.wl[16 * k:16 * k + 16, :], T.want[:, :]).then_inc(sem["ld_w"], 16)
    SY.dma_start(T.vt[:, :], T.v[:, :]).then_inc(sem["ld_v"], 16)
    for k in range(8):
        (S, SY)[k % 2].dma_start(T.sw[16 * k:16 * k + 16, :], T.slot[:, :]).then_inc(sem["ld_s"], 16)
    SY.dma_start(T.at[:, :], T.a[:, :]).then_inc(sem["ld_a"], 16)

    g.iota(T.ec[:, :], [[0, 2]], 0, 4, allow_small_or_imprecise_dtypes=True).then_inc(sem["itc"], 1)
    g.iota(T.ea[:, :], [[1, 128]], 0, 0, allow_small_or_imprecise_dtypes=True).then_inc(sem["ita"], 1)
    g.iota(T.eb[:, :], [[1, 32], [64, 4]], 0, 0, allow_small_or_imprecise_dtypes=True).then_inc(sem["itb"], 1)

    off_eng = topo.engines(core, T.cores[at(1)[0]])
    spare = [e for e in topo.engines(core, T.cores[nbr]) if e not in off_eng][::2][:2]
    sent = [0]

    def engines(lo, hi, thin=False):
        far = [i for i in range(lo, hi) if ORDER[i][0]]
        eng = off_eng[::2] if thin else off_eng
        n = len(eng) // max(len(far), 1)
        return {i: eng[n * far.index(i):n * far.index(i) + n] if i in far else spare for i in range(lo, hi)}

    def send(lo, hi, item, thin=False):
        trs = []
        for i, es in engines(lo, hi, thin).items():
            r, s, d, x = item(i)
            rid, pid, _ = topo.addr(T.cores[r])
            trs.append(RemoteDMATransfer(dst_ids=[DstId(rid=rid, pnc=pid)], dma_engine_mask=sum(1 << e for e in es),
                                         remote_sem=sem[s], srcs=[x], dsts=[d], alu_op=0))
            sent[0] += len(es)
        g.remote_dma_fused(trs, local_sem=sem["sent"])

    g.wait_ge(sem["cv"], 2)
    for k, (lo, hi) in enumerate(LISTS):
        send(lo, hi, lambda i: (servers[i], "l%d" % k, T.lst[:, 4 * i:4 * i + 4], T.loff[:, 4 * servers[i]:4 * servers[i] + 4]), k == 0)

    for lo, hi in SENDS:
        for b, (x, z) in enumerate(BATCHES):
            if x <= lo < z:
                g.wait_ge(sem["q%d" % b], 1)
        for K, R_, view in ((T.k, T.r, lambda buf, c: buf[:, c:c + 64].bitcast(dt.uint8)), (T.ks, T.rs, lambda buf, c: buf[:, c:c + 64])):
            send(lo, hi, lambda i: (dests[i], "arr%d" % ORDER[i][0],
                                    view(R_, 128 * (nch - 1 - ORDER[i][0]) + 64 * par) if ORDER[i][0] else view(K, 128 * par), view(K, kcol[i])))
    g.wait_ge(sem["sent"], sent[0])

    def arrived(d):
        return sum(2 * len(es) for lo, hi in SENDS for i, es in engines(lo, hi).items() if ORDER[i][0] == d)

    def copy(q, out, in_, s):
        if q == "v":
            V.tensor_copy(out, in_).then_inc(sem[s], 1)
        else:
            S.activation(out, in_, COPY).then_inc(sem[s], 1)

    def wait(q, *pairs):
        for s, n in pairs:
            (V if q == "v" else S).wait_ge(sem[s], n)

    def ones(o):
        for t in range(4):
            V.tensor_scalar(T.idt[:, 512 * o + t:512 * o + 512:4], (T.eb if o < 2 else T.ea)[:, :], float((32 if o < 2 else 128) * o - t),
                            T.ec[:, 0:1], A.add, A.is_equal).then_inc(sem["eb"], 1)

    for x in zeros:
        V.memset(T.gt[:, 4 * x:4 * x + 256], 0.0).then_inc(sem["gz"], 1)
    wait("v", ("gz", len(zeros)), ("itc", 1), ("ita", 1))
    wait("v", ("ld_w", 64))
    for hf in range(2):
        V.tensor_scalar(T.loff[64 * hf:64 * hf + 64, :], T.wl[:, :], 0, 4, A.max, A.mult).then_inc(sem["cv"], 1)
    ones(2)
    ones(3)
    wait("v", ("itb", 1))
    ones(0)
    ones(1)
    wait("v", ("ld_s", 128))
    V.tensor_scalar(T.s1i[:, :], T.sw[:, :], 128 * me, 640, A.is_lt, A.mult).then_inc(sem["sa"], 1)
    wait("v", ("eb", 16))
    V.quantize_mx(T.eq[:, :], T.eqs[:, :], T.idt[:, :]).then_inc(sem["eqd"], 1)
    wait("v", ("sa", 1))
    V.tensor_tensor(T.s2i[:, :], T.s1i[:, :], T.sw[:, :], A.add).then_inc(sem["sb"], 1)

    wait("s", ("ld_v", 16), ("cv", 2))
    for t in range(4):
        copy("s", T.gt[:, 4 * own + t:4 * own + 256:4], T.vt[:, t:2048].indirect(T.loff[:, 4 * rank:4 * rank + 4]), "go")
    wait("v", ("ld_v", 16), ("go", 4))

    def codes(b, c0, n, nv, ns):
        wait("v", ("gav%d" % b, nv), ("gas%d" % b, ns))
        V.quantize_mx(T.k[:, c0:c0 + n], T.ks[:, c0:c0 + n], T.gt[:, 4 * c0:4 * (c0 + n)]).then_inc(sem["q%d" % b], 1)

    held = []
    for b, (lo, hi) in enumerate(BATCHES):
        c0, n = kcol[lo], 64 * (hi - lo)
        cut = n - HELP[b]
        parts = {"v": [(0, 0, n)] + ([(1, 0, cut)] if cut else []), "s": [(2, 0, n), (3, 0, n)] + ([(1, cut, n)] if cut < n else [])}
        for q in "vs":
            wait(q, *[("l%d" % k, sum(len(es) for es in engines(x, z, k == 0).values())) for k, (x, z) in enumerate(LISTS) if x < hi and lo < z])
            for t, x, z in parts[q]:
                copy(q, T.gt[:, 4 * (c0 + x) + t:4 * (c0 + z):4], T.vt[:, t:2048].indirect(T.lst[:, 4 * lo + x // 16:4 * lo + z // 16]),
                     "ga%s%d" % (q, b))
                if q == "v" and held:
                    codes(*held.pop())
        held.append((b, c0 if b else min(first, own), max(n, 128), len(parts["v"]), len(parts["s"])))
        if b not in HOLD:
            codes(*held.pop())

    wait("v", ("sb", 1))
    V.tensor_scalar(T.sl[:, :], T.s2i[:, :], 128 * me, None, A.subtract).then_inc(sem["sl"], 1)
    for k in range(4):
        for o in range(2):
            V.tensor_scalar(T.slx[:, 16 * k + 8 * o:16 * k + 8 * o + 8], T.s2i[:, 8 * k:8 * k + 8], 640 * o - 128 * me, None,
                            A.add).then_inc(sem["sl"], 1)
    V.tensor_scalar(T.idn[:, :], T.ea[:, :], 4.0, T.ec[:, 0:1], A.mult, A.is_equal).then_inc(sem["idn"], 1)
    wait("v", ("ld_a", 16))
    V.quantize_mx(T.aq[:, :], T.aqs[:, :], T.at[:, :]).then_inc(sem["qa"], 1)

    def P(k, n):
        return T.ps[:, 512 * k:512 * k + n]

    nr = len(ROUNDS)
    hi_, lo_ = 4 * ((nr - 1) % 2), 4 * (nr % 2)
    results = {0: (lo_ + 1, "c%d_1" % (nr - 2), 0, 0, 256), 1: (lo_ + 3, "c%d_3" % (nr - 2), 1, 0, 256),
               2: (lo_ + 2, "c%d_2" % (nr - 2), 2, 0, 256), 3: (lo_, "hc2", 3, 0, 128), 4: (hi_, "hp0", 3, 128, 128)}

    def unpack(i, *os_):
        ds = ROUNDS[i]
        for d in ds:
            PE.wait_ge(sem["arr%d" % d], arrived(d))
        x, n = 128 * (nch - 1 - ds[-1]), 128 * len(ds)
        codes, plane = (T.r[:, x:x + n], T.rs[:, x:x + n]) if ds[0] else (T.k[:, pair:pair + 128], T.ks[:, pair:pair + 128])
        for o in os_:
            if i >= 2:
                PE.wait_ge(sem["c%d_%d" % (i - 2, o)], 1)
            PE.matmul_mx(P(4 * (i % 2) + o, n), T.eq[:, 128 * o:128 * o + 128], T.eqs[:, 128 * o:128 * o + 128], codes, plane,
                         True, True).then_inc(sem["m%d_%d" % (i, o)], 1)

    def product(i):
        bank, free, o, x, n = results[i]
        PE.wait_ge(sem[free], 1)
        PE.wait_ge(sem["hq%d" % (o if o > 1 else 0)], 1)
        PE.matmul_mx(P(bank, n), T.hq[:, 128 * o:128 * o + 128], T.hqs[:, 128 * o:128 * o + 128],
                     T.aq[:, x:x + n], T.aqs[:, x:x + n], True, True).then_inc(sem["ym%d" % i], 1)

    def turn(o, t):
        if t == 0:
            PE.wait_ge(sem["gv%d" % o], 1)
            PE.wait_ge(sem["gs%d" % o], 1)
        if o == 2:
            PE.wait_ge(sem["c%d_0" % (nr - 2)], 1)
            PE.transpose(T.ps[:, 512 * lo_ + t:512 * lo_ + 512:4], T.g2[:, t:512:4], T.idn[:, :]).then_inc(sem["tr2"], 1)
        else:
            PE.wait_ge(sem["c%d_%d" % (nr - 1, t)], 1)
            PE.transpose(P(hi_ + t, 128), T.g3[:, t:512:4], T.idn[:, :]).then_inc(sem["tt%d" % t], 1)

    PE.wait_ge(sem["eqd"], 1)
    PE.wait_ge(sem["q0"], 1)
    for i in range(nr - 1):
        unpack(i, 2, 3, 0, 1)
    PE.wait_ge(sem["idn"], 1)
    PE.wait_ge(sem["qa"], 1)
    for step in TAIL["tensor"].split():
        n = [int(x) for x in step[1:]]
        {"u": lambda *os_: unpack(nr - 1, *os_), "t": turn, "y": product}[step[0]](*n)

    def unpacked(q, o, i=nr - 1):
        ds = ROUNDS[i]
        x, n = 640 * o + 128 * ((nch - ds[-1]) % nch), 128 * len(ds)
        wait(q, ("m%d_%d" % (i, o), 1))
        copy(q, T.w[:, x:x + n], P(4 * (i % 2) + o, n), "c%d_%d" % (i, o))

    def choose(q, o):
        wait(q, ("sl", 9), *[("c%d_%d" % (i, o), 1) for i in range(nr)])
        x, z = (0, CUT[o]) if q == "v" else (CUT[o], 512)
        copy(q, T["g%d" % o][:, x:z], T.w[:, 640 * o:640 * o + 640].indirect(T.sl[:, x // 16:z // 16]), "g%s%d" % (q, o))

    def quarter(q, k):
        wait(q, ("sl", 9), *[("c%d_%d" % (i, o), 1) for i in range(nr) for o in (0, 1)])
        copy(q, T.gd[:, 256 * k:256 * k + 256], T.w[:, 0:1280].indirect(T.slx[:, 16 * k:16 * k + 16]), "gd%d" % k)

    def squares(q, o):
        wait("v", ("xd", 64))
        for t in range(4):
            V.transpose(T.ht[:, t:1024:4], T.xd[:, t:1024:4]).then_inc(sem["hc0"], 1)

    def block(q, o):
        wait(q, ("tr2", 4))
        copy(q, T.ht[:, 1024:1536], P(lo_, 512), "hc2")

    def piece(q, t):
        wait(q, ("tt%d" % t, 1))
        copy(q, T.ht[:, 1536 + t:2048:4], P(hi_ + t, 128), "hp%d" % t)

    made = {0: [("hc0", 4)], 2: [("hc2", 1)], 3: [("hp%d" % t, 1) for t in range(4)]}
    end = {0: 2, 2: 3, 3: 4}

    def quant(q, o):
        wait("v", *made[o])
        V.quantize_mx(T.hq[:, 128 * o:128 * end[o]], T.hqs[:, 128 * o:128 * end[o]], T.ht[:, 512 * o:512 * end[o]]).then_inc(sem["hq%d" % o], 1)

    def result(q, i):
        bank, _, o, x, n = results[i]
        wait(q, ("ym%d" % i, 1))
        copy(q, T.yt[:, 256 * o + x:256 * o + x + n], P(bank, n), "yc%d" % i)

    for q in "vs":
        for i in range(nr - 1):
            for o in EARLY[q][i]:
                unpacked(q, o, i)
        for step in TAIL[q].split():
            {"c": unpacked, "g": choose, "k": quarter, "s": squares, "b": block, "p": piece, "q": quant, "y": result}[step[0]](q, int(step[1]))

    def exchange(k):
        SY.wait_ge(sem["gd%d" % k], 1)
        SY.dma_start(T.xd[32 * k:32 * k + 32, :], T.gd[:, 256 * k:256 * k + 256]).then_inc(sem["xd"], 16)

    def store_h(o):
        for s, n in made[o]:
            SY.wait_ge(sem[s], n)
        SY.dma_start(T.h[:, 512 * o:512 * end[o]], T.ht[:, 512 * o:512 * end[o]]).then_inc(sem["stored"], 16)

    def store_y(o):
        for i in results:
            if results[i][2] == o:
                SY.wait_ge(sem["yc%d" % i], 1)
        SY.dma_start(T.y[:, 256 * o:256 * o + 256], T.yt[:, 256 * o:256 * o + 256]).then_inc(sem["stored"], 16)

    for step in TAIL["sync"].split():
        {"x": exchange, "h": store_h, "y": store_y}[step[0]](int(step[1]))
    SY.wait_ge(sem["stored"], 112)
